import numpy as np
import ml_dtypes


def mxq(x, axis, fmt="e4m3"):
    dtype, down = {"e4m3": (ml_dtypes.float8_e4m3fn, 7), "e5m2": (ml_dtypes.float8_e5m2, 14)}[fmt]
    v = np.moveaxis(np.asarray(x, np.float32).astype(ml_dtypes.bfloat16).astype(np.float64), axis, -1)
    blocks = v.reshape(v.shape[:-1] + (-1, 32))
    amax = np.abs(blocks).max(-1, keepdims=True)
    byte = np.maximum(np.where(amax > 0, np.frexp(amax)[1] - 1 + 127, 0) - down, 1)
    scale = np.exp2(byte - 127.0)
    codes = (blocks / scale).astype(np.float32).astype(dtype).astype(np.float64)
    return np.moveaxis((codes * scale).reshape(v.shape), -1, axis)


WIDE = False


def mx_kscale(k):
    if not WIDE:
        return np.ones(k)
    levels = np.array([10, -10, 5, -5, 0])
    if k % 512:
        return np.exp2(np.random.permutation(np.resize(levels, k // 32))).repeat(32)
    a = np.empty((k // 512, 16))
    for p in range(k // 512):
        a[p, :8] = np.random.permutation(np.resize(levels, 8))
        for g in range(8):
            far = levels[np.abs(levels - a[p, g]) >= 10]
            a[p, g + 8] = far[np.random.randint(len(far))]
    return np.exp2(a.ravel()).repeat(32)


def f64(x):
    return np.asarray(x).astype(np.float64)


def striped(idx):
    return np.tile(idx.reshape(-1, 16).T, (8, 1)).astype(np.uint16)


def unstriped(offs):
    return offs[:16].T.reshape(-1).astype(np.int64)


E2M1 = np.array([0.0, 0.5, 1.0, 1.5, 2.0, 3.0, 4.0, 6.0, -0.0, -0.5, -1.0, -1.5, -2.0, -3.0, -4.0, -6.0])


def pack_weight(w, fmt):
    k, n = w.shape
    w = f64(np.asarray(w, np.float32).astype(ml_dtypes.bfloat16)).reshape(k // 32, 32, n)
    amax = np.abs(w).max(1)
    if fmt == "e4m3":
        byte = np.frexp(amax)[1] - 1 + 127 - 7
    else:
        mant, ex = np.frexp(amax / 6.0)
        byte = np.where(mant > 0.5, ex, ex - 1) + 127
    byte = np.clip(np.where(amax > 0, byte, 1), 1, 254)
    scaled = (w * np.exp2(127.0 - byte)[:, None, :]).reshape(k, n).astype(np.float32)
    by_word = np.ascontiguousarray(scaled.reshape(k // 512, 128, 4, n).transpose(0, 1, 3, 2))
    if fmt == "e4m3":
        words = by_word.astype(ml_dtypes.float8_e4m3fn).view(np.uint8)
    else:
        c = by_word.astype(ml_dtypes.float4_e2m1fn).view(np.uint8) & 0xF
        words = (c[..., 0::2] | (c[..., 1::2] << 4)).reshape(k // 512, 128, 2 * n)
    return np.ascontiguousarray(words), np.ascontiguousarray(byte.astype(np.uint8).reshape(k // 512, 16, n))


def unpack_weight(words, scales, fmt):
    g, _, n = scales.shape
    words = np.ascontiguousarray(words).reshape(g, 128, n, -1)
    if fmt == "e4m3":
        vals = words.view(ml_dtypes.float8_e4m3fn).astype(np.float64)
    else:
        nib = np.empty((g, 128, n, 4), np.uint8)
        nib[..., 0::2] = words & 0xF
        nib[..., 1::2] = words >> 4
        vals = E2M1[nib]
    vals = vals * np.repeat(np.exp2(scales.astype(np.float64) - 127.0), 8, axis=1)[..., None]
    return vals.transpose(0, 1, 3, 2).reshape(g * 512, n)


def gelu(v):
    return 0.5 * v * (1.0 + np.tanh(np.sqrt(2.0 / np.pi) * (v + 0.044715 * v**3)))


K, T, E, C, N = 512, 4096, 16, 128, 128


def by_expert(wq, xq):
    return np.concatenate([wq[e].T @ xq[:, e * C:(e + 1) * C] for e in range(E)], axis=1)


def setup_inputs():
    n = np.random.standard_normal
    s = mx_kscale(K)[:, None]
    w = [pack_weight(m, "e2m1") for m in n((E, K, N)) / np.sqrt(K) / s[None]]
    return {
        "xT": (n((K, T)) * s).astype(np.float32),
        "w_words": np.stack([m[0] for m in w]),
        "w_scales": np.stack([m[1] for m in w]),
        "b": (0.3 * n((N, E))).astype(np.float32),
        "gate": np.tile(np.random.uniform(0.2, 1.0, E * C), (N, 1)).astype(np.float32),
        "offs": striped(np.random.permutation(T)[:E * C]),
        "dst": striped(np.random.permutation(T)[:E * C]),
    }


def reference(xT, w_words, w_scales, b, gate, offs, dst):
    idx = unstriped(offs)
    w = np.stack([unpack_weight(w_words[e], w_scales[e], "e2m1") for e in range(E)])
    xq = mxq(f64(xT)[:, idx], 0, "e4m3")
    y = by_expert(w, xq)
    y = gelu(y + np.repeat(f64(b), C, axis=1))
    out = np.zeros((N, T))
    out[:, unstriped(dst)] = f64(gate) * y
    return out

@@ -1,0 +1,148 @@
+import concourse.mybir as mybir
+
+T, E, SLOTS, N = 4096, 16, 2048, 128
+FLOPS = 2 * SLOTS * 512 * N
+
+F32 = mybir.dt.float32
+BF16 = mybir.dt.bfloat16
+I32 = mybir.dt.int32
+U32 = mybir.dt.uint32
+U16 = mybir.dt.uint16
+U8 = mybir.dt.uint8
+FP8X4 = mybir.dt.float8_e4m3fn_x4
+FP4X4 = mybir.dt.float4_e2m1fn_x4
+
+P = 128
+G = 512
+A, B, C, D = range(4)
+CHUNKS = (((0, 2048), (2048, 3072), (3072, 4096)), ((0, 1536), (1536, 3072), (3072, 3584), (3584, 4096)))
+CASTS = (
+    (("v", 0, 1280), ("s", 1280, 2048), ("v", 2048, 3072), ("v", 3072, 3712), ("s", 3712, 4096)),
+    (("s", 0, 1536), ("s", 1536, 2048), ("v", 2048, 3072), ("s", 3072, 3584), ("v", 3584, 3840), ("s", 3840, 4096)),
+)
+
+
+def tile_moe_two_lin_gelu_kernel(tc, xT, w_words, w_scales, b, gate, offs, dst, out):
+    nc = tc.nc
+    gelu = mybir.ActivationFunctionType.Gelu_apprx_tanh
+    mult = mybir.AluOpType.mult
+
+    with tc.tile_pool(name="keep", bufs=1) as keep, tc.psum_pool(name="psum", bufs=1) as psum:
+        offs_t = keep.tile([P, SLOTS // 16], U16, name="offs_t")
+        dst_t = keep.tile([P, SLOTS // 16], U16, name="dst_t")
+        raw_0 = keep.tile([P, 2, T], F32, name="raw_0")
+        raw_1 = [keep.tile([P, 2, c1 - c0], F32, name=f"raw_1_{c0}") for c0, c1 in CHUNKS[1]]
+        words = [keep.tile([P, 2 * T], BF16, name=f"words{u}", align_bytes=64) for u in range(2)]
+        grouped_ab = keep.tile([P, 8 * G], BF16, name="grouped_ab", align_bytes=64)
+        grouped_cd = keep.tile([P, 8 * G], BF16, name="grouped_cd", align_bytes=64)
+        codes = keep.tile([P, SLOTS], U32, name="codes", align_bytes=64)
+        late_cd = keep.tile([P, 4 * G], BF16, name="late_cd", align_bytes=64)
+        scales = keep.tile([P, SLOTS], U8, name="scales", align_bytes=64)
+        w_t = keep.tile([P, E, 2 * N], U8, name="w_t", align_bytes=64)
+        ws_t = keep.tile([P, E, N], U8, name="ws_t", align_bytes=64)
+        b_t = keep.tile([P, E], F32, name="b_t")
+        gate_t = [keep.tile([P, n], F32, name=f"gate{i}") for i, n in enumerate((G, 3 * G))]
+        y_a = keep.tile([P, G], F32, name="y_a")
+        y_bcd = keep.tile([P, 3 * G], F32, name="y_bcd")
+        out_t = keep.tile([P, T], F32, name="out_t")
+        warm = keep.tile([P, 1], F32, name="warm")
+        acc = [psum.tile([P, G], F32, name=f"acc{g}") for g in range(4)]
+
+        x_rows = xT.rearrange("(p t) w -> p t w", t=4)
+        ws_rows = w_scales.bitcast(I32).rearrange("e a q n -> (a q) e n")
+        w_rows = w_words.bitcast(I32).rearrange("e a p n -> p (e a) n")
+
+        def load_weights(e0, e1):
+            for q in range(4):
+                nc.sync.dma_start(out=ws_t[32 * q : 32 * q + 4, e0:e1, :].bitcast(I32), in_=ws_rows[4 * q : 4 * q + 4, e0:e1])
+            nc.sync.dma_start(out=w_t[:, e0:e1, :].bitcast(I32), in_=w_rows[:, e0:e1, :])
+
+        nc.vector.memset(warm[:], 0.0)
+        nc.scalar.activation(out=warm[:], in_=warm[:], func=gelu)
+        nc.vector.memset(ws_t[:].rearrange("p e n -> p (e n)").bitcast(I32), 0)
+        nc.gpsimd.memset(out_t[:], 0.0)
+
+        nc.sync.dma_start(out=raw_0[:, 0, :], in_=x_rows[:, 0, :])
+        nc.sync.dma_start(offs_t[:], offs)
+        for c0, c1 in CHUNKS[0]:
+            nc.sync.dma_start(out=raw_0[:, 1, c0:c1], in_=x_rows[:, 1, c0:c1])
+        for i, (c0, c1) in enumerate(CHUNKS[1]):
+            nc.sync.dma_start(out=raw_1[i][:], in_=x_rows[:, 2:4, c0:c1])
+        load_weights(0, 4)
+        nc.sync.dma_start(b_t[:], b)
+        load_weights(4, E)
+        nc.sync.dma_start(dst_t[:], dst)
+        for i, (s0, s1) in enumerate(((0, G), (G, 4 * G))):
+            nc.sync.dma_start(out=gate_t[i][:], in_=gate[:, s0:s1])
+
+        def slots(grouped, s0, s1):
+            return grouped[:, 4 * s0 : 4 * s1].rearrange("p (n t) -> p n t", t=4)
+
+        def cast(u, engine, c0, c1):
+            if u == 0:
+                raw = raw_0[:, :, c0:c1]
+            else:
+                i = [c[0] <= c0 and c1 <= c[1] for c in CHUNKS[1]].index(True)
+                base = CHUNKS[1][i][0]
+                raw = raw_1[i][:, :, c0 - base : c1 - base]
+            to = words[u][:, 2 * c0 : 2 * c1].rearrange("p (n t) -> p n t", t=2)
+            src = raw.rearrange("p t n -> p n t")
+            if engine == "v":
+                nc.vector.tensor_copy(out=to, in_=src)
+            else:
+                nc.scalar.copy(out=to, in_=src)
+
+        def gather(to, u, s0, s1):
+            nc.vector.tensor_copy(to, words[u][:].bitcast(U32).indirect(offs_t[:, s0 // 16 : s1 // 16]))
+
+        def stepped(grouped, u):
+            return grouped[:].bitcast(U32).rearrange("p (n u) -> p u n", u=2)[:, u, :]
+
+        def merge(grouped, late, s0, s1):
+            nc.scalar.copy(out=slots(grouped, s0, s1)[:, :, 2:4], in_=late[:, 2 * s0 : 2 * s1].rearrange("p (n t) -> p n t", t=2))
+
+        def quantize(grouped, s0, s1):
+            nc.vector.quantize_mx(out=codes[:, s0:s1].bitcast(FP8X4), scales=scales[:, s0:s1], in_=grouped)
+
+        def multiply(g, y, y_base):
+            for pass_kind in ("matmul", "gelu"):
+                for i in range(4):
+                    e = 4 * g + i
+                    a = acc[g][:, i * N : (i + 1) * N]
+                    if pass_kind == "matmul":
+                        nc.tensor.matmul_mx(
+                            out=a,
+                            lhsT=w_t[:, e, :].bitcast(FP4X4),
+                            lhsT_scale=ws_t[:, e, :],
+                            rhs=codes[:, e * N : (e + 1) * N].bitcast(FP8X4),
+                            rhs_scale=scales[:, e * N : (e + 1) * N],
+                            start=True,
+                            stop=True,
+                        )
+                    else:
+                        nc.scalar.activation(out=y[:, e * N - y_base : (e + 1) * N - y_base], in_=a, func=gelu, bias=b_t[:, e : e + 1])
+
+        def scatter(i, y, s0, s1):
+            nc.vector.tensor_tensor(out_t[:].indirect(dst_t[:, s0 // 16 : s1 // 16]), y[:], gate_t[i][:], mult)
+
+        for c in CASTS[0]:
+            cast(0, *c)
+        gather(stepped(grouped_ab, 0), 0, 0, 2 * G)
+        gather(stepped(grouped_cd, 0), 0, 2 * G, 4 * G)
+        for c in CASTS[1]:
+            cast(1, *c)
+        gather(late_cd[:].bitcast(U32), 1, 2 * G, 4 * G)
+        merge(grouped_cd, late_cd, 0, G)
+        merge(grouped_cd, late_cd, G, 2 * G)
+        gather(stepped(grouped_ab, 1)[:, 0:G], 1, 0, G)
+        gather(stepped(grouped_ab, 1)[:, G : 2 * G], 1, G, 2 * G)
+        quantize(grouped_ab[:, 0 : 4 * G], 0, G)
+        multiply(A, y_a, 0)
+        quantize(grouped_ab[:, 4 * G : 8 * G], G, 2 * G)
+        multiply(B, y_bcd, G)
+        quantize(grouped_cd[:], 2 * G, 4 * G)
+        multiply(C, y_bcd, G)
+        multiply(D, y_bcd, G)
+        scatter(0, y_a, 0, G)
+        scatter(1, y_bcd, G, 4 * G)
+        nc.sync.dma_start(out, out_t[:])

@@ -13,136 +13,91 @@ FP8X4 = mybir.dt.float8_e4m3fn_x4
 FP4X4 = mybir.dt.float4_e2m1fn_x4
 
 P = 128
-G = 512
-A, B, C, D = range(4)
-CHUNKS = (((0, 2048), (2048, 3072), (3072, 4096)), ((0, 1536), (1536, 3072), (3072, 3584), (3584, 4096)))
-CASTS = (
-    (("v", 0, 1280), ("s", 1280, 2048), ("v", 2048, 3072), ("v", 3072, 3712), ("s", 3712, 4096)),
-    (("s", 0, 1536), ("s", 1536, 2048), ("v", 2048, 3072), ("s", 3072, 3584), ("v", 3584, 3840), ("s", 3840, 4096)),
-)
+VECTOR_SLOTS = (640, 640, 1024, 1024)
+CUTS = ((0, 2048, 3584, 4096), (0, 2048, 3328, 4096), (0, 2048, 3328, 4096), (0, 1792, 3328, 4096))
+SCALAR_CASTS = ((3904, 4096), (0, 0), (0, 0), (1792, 3328))
+QUANT = ((0, 1024), (1024, 2048))
+SCATTERS = ((0, 512), (512, 2048))
 
 
 def tile_moe_two_lin_gelu_kernel(tc, xT, w_words, w_scales, b, gate, offs, dst, out):
     nc = tc.nc
     gelu = mybir.ActivationFunctionType.Gelu_apprx_tanh
+    copy = mybir.ActivationFunctionType.Copy
     mult = mybir.AluOpType.mult
 
     with tc.tile_pool(name="keep", bufs=1) as keep, tc.psum_pool(name="psum", bufs=1) as psum:
         offs_t = keep.tile([P, SLOTS // 16], U16, name="offs_t")
         dst_t = keep.tile([P, SLOTS // 16], U16, name="dst_t")
-        raw_0 = keep.tile([P, 2, T], F32, name="raw_0")
-        raw_1 = [keep.tile([P, 2, c1 - c0], F32, name=f"raw_1_{c0}") for c0, c1 in CHUNKS[1]]
-        words = [keep.tile([P, 2 * T], BF16, name=f"words{u}", align_bytes=64) for u in range(2)]
-        grouped_ab = keep.tile([P, 8 * G], BF16, name="grouped_ab", align_bytes=64)
-        grouped_cd = keep.tile([P, 8 * G], BF16, name="grouped_cd", align_bytes=64)
+        raw = [keep.tile([P, T], F32, name=f"raw{t}") for t in range(4)]
+        half = [keep.tile([P, T], BF16, name=f"half{t}") for t in range(4)]
+        grouped = keep.tile([P, 4 * SLOTS], BF16, name="grouped", align_bytes=64)
         codes = keep.tile([P, SLOTS], U32, name="codes", align_bytes=64)
-        late_cd = keep.tile([P, 4 * G], BF16, name="late_cd", align_bytes=64)
         scales = keep.tile([P, SLOTS], U8, name="scales", align_bytes=64)
         w_t = keep.tile([P, E, 2 * N], U8, name="w_t", align_bytes=64)
         ws_t = keep.tile([P, E, N], U8, name="ws_t", align_bytes=64)
         b_t = keep.tile([P, E], F32, name="b_t")
-        gate_t = [keep.tile([P, n], F32, name=f"gate{i}") for i, n in enumerate((G, 3 * G))]
-        y_a = keep.tile([P, G], F32, name="y_a")
-        y_bcd = keep.tile([P, 3 * G], F32, name="y_bcd")
+        gate_t = [keep.tile([P, s1 - s0], F32, name=f"gate{s0}") for s0, s1 in SCATTERS]
+        y = keep.tile([P, SLOTS], F32, name="y")
         out_t = keep.tile([P, T], F32, name="out_t")
         warm = keep.tile([P, 1], F32, name="warm")
-        acc = [psum.tile([P, G], F32, name=f"acc{g}") for g in range(4)]
+        acc = [psum.tile([P, 512], F32, name=f"acc{g}") for g in range(4)]
 
         x_rows = xT.rearrange("(p t) w -> p t w", t=4)
         ws_rows = w_scales.bitcast(I32).rearrange("e a q n -> (a q) e n")
         w_rows = w_words.bitcast(I32).rearrange("e a p n -> p (e a) n")
 
-        def load_weights(e0, e1):
-            for q in range(4):
-                nc.sync.dma_start(out=ws_t[32 * q : 32 * q + 4, e0:e1, :].bitcast(I32), in_=ws_rows[4 * q : 4 * q + 4, e0:e1])
-            nc.sync.dma_start(out=w_t[:, e0:e1, :].bitcast(I32), in_=w_rows[:, e0:e1, :])
-
         nc.vector.memset(warm[:], 0.0)
         nc.scalar.activation(out=warm[:], in_=warm[:], func=gelu)
         nc.vector.memset(ws_t[:].rearrange("p e n -> p (e n)").bitcast(I32), 0)
-        nc.gpsimd.memset(out_t[:], 0.0)
+        nc.vector.memset(out_t[:], 0.0)
 
-        nc.sync.dma_start(out=raw_0[:, 0, :], in_=x_rows[:, 0, :])
-        nc.sync.dma_start(offs_t[:], offs)
-        for c0, c1 in CHUNKS[0]:
-            nc.sync.dma_start(out=raw_0[:, 1, c0:c1], in_=x_rows[:, 1, c0:c1])
-        for i, (c0, c1) in enumerate(CHUNKS[1]):
-            nc.sync.dma_start(out=raw_1[i][:], in_=x_rows[:, 2:4, c0:c1])
-        load_weights(0, 4)
+        for t in range(4):
+            for i in range(len(CUTS[t]) - 1):
+                c0, c1 = CUTS[t][i : i + 2]
+                nc.sync.dma_start(out=raw[t][:, c0:c1], in_=x_rows[:, t, c0:c1])
+                if t == 0 and i == 0:
+                    nc.sync.dma_start(offs_t[:], offs)
+        for q in range(4):
+            nc.sync.dma_start(out=ws_t[32 * q : 32 * q + 4, :, :].bitcast(I32), in_=ws_rows[4 * q : 4 * q + 4, :])
+        nc.sync.dma_start(out=w_t[:].bitcast(I32), in_=w_rows)
         nc.sync.dma_start(b_t[:], b)
-        load_weights(4, E)
         nc.sync.dma_start(dst_t[:], dst)
-        for i, (s0, s1) in enumerate(((0, G), (G, 4 * G))):
+        for i, (s0, s1) in enumerate(SCATTERS):
             nc.sync.dma_start(out=gate_t[i][:], in_=gate[:, s0:s1])
 
-        def slots(grouped, s0, s1):
-            return grouped[:, 4 * s0 : 4 * s1].rearrange("p (n t) -> p n t", t=4)
+        planes = grouped[:].rearrange("p (n t) -> p t n", t=4)
 
-        def cast(u, engine, c0, c1):
-            if u == 0:
-                raw = raw_0[:, :, c0:c1]
-            else:
-                i = [c[0] <= c0 and c1 <= c[1] for c in CHUNKS[1]].index(True)
-                base = CHUNKS[1][i][0]
-                raw = raw_1[i][:, :, c0 - base : c1 - base]
-            to = words[u][:, 2 * c0 : 2 * c1].rearrange("p (n t) -> p n t", t=2)
-            src = raw.rearrange("p t n -> p n t")
-            if engine == "v":
-                nc.vector.tensor_copy(out=to, in_=src)
-            else:
-                nc.scalar.copy(out=to, in_=src)
+        for t in range(4):
+            lo, hi = SCALAR_CASTS[t]
+            edges = sorted(set(CUTS[t]) | {lo, hi})
+            for c0, c1 in zip(edges, edges[1:]):
+                if lo <= c0 and c1 <= hi:
+                    nc.scalar.copy(out=half[t][:, c0:c1], in_=raw[t][:, c0:c1])
+                else:
+                    nc.vector.tensor_copy(out=half[t][:, c0:c1], in_=raw[t][:, c0:c1])
+            v = VECTOR_SLOTS[t]
+            nc.vector.tensor_copy(planes[:, t, :v], raw[t][:].indirect(offs_t[:, : v // 16]))
+            nc.scalar.activation(planes[:, t, v:], half[t][:].indirect(offs_t[:, v // 16 :]), copy)
 
-        def gather(to, u, s0, s1):
-            nc.vector.tensor_copy(to, words[u][:].bitcast(U32).indirect(offs_t[:, s0 // 16 : s1 // 16]))
+        for s0, s1 in QUANT:
+            nc.vector.quantize_mx(out=codes[:, s0:s1].bitcast(FP8X4), scales=scales[:, s0:s1], in_=grouped[:, 4 * s0 : 4 * s1])
+        for g in range(4):
+            for i in range(4):
+                e = 4 * g + i
+                nc.tensor.matmul_mx(
+                    out=acc[g][:, i * N : (i + 1) * N],
+                    lhsT=w_t[:, e, :].bitcast(FP4X4),
+                    lhsT_scale=ws_t[:, e, :],
+                    rhs=codes[:, e * N : (e + 1) * N].bitcast(FP8X4),
+                    rhs_scale=scales[:, e * N : (e + 1) * N],
+                    start=True,
+                    stop=True,
+                )
+            for i in range(4):
+                e = 4 * g + i
+                nc.scalar.activation(out=y[:, e * N : (e + 1) * N], in_=acc[g][:, i * N : (i + 1) * N], func=gelu, bias=b_t[:, e : e + 1])
 
-        def stepped(grouped, u):
-            return grouped[:].bitcast(U32).rearrange("p (n u) -> p u n", u=2)[:, u, :]
-
-        def merge(grouped, late, s0, s1):
-            nc.scalar.copy(out=slots(grouped, s0, s1)[:, :, 2:4], in_=late[:, 2 * s0 : 2 * s1].rearrange("p (n t) -> p n t", t=2))
-
-        def quantize(grouped, s0, s1):
-            nc.vector.quantize_mx(out=codes[:, s0:s1].bitcast(FP8X4), scales=scales[:, s0:s1], in_=grouped)
-
-        def multiply(g, y, y_base):
-            for pass_kind in ("matmul", "gelu"):
-                for i in range(4):
-                    e = 4 * g + i
-                    a = acc[g][:, i * N : (i + 1) * N]
-                    if pass_kind == "matmul":
-                        nc.tensor.matmul_mx(
-                            out=a,
-                            lhsT=w_t[:, e, :].bitcast(FP4X4),
-                            lhsT_scale=ws_t[:, e, :],
-                            rhs=codes[:, e * N : (e + 1) * N].bitcast(FP8X4),
-                            rhs_scale=scales[:, e * N : (e + 1) * N],
-                            start=True,
-                            stop=True,
-                        )
-                    else:
-                        nc.scalar.activation(out=y[:, e * N - y_base : (e + 1) * N - y_base], in_=a, func=gelu, bias=b_t[:, e : e + 1])
-
-        def scatter(i, y, s0, s1):
-            nc.vector.tensor_tensor(out_t[:].indirect(dst_t[:, s0 // 16 : s1 // 16]), y[:], gate_t[i][:], mult)
-
-        for c in CASTS[0]:
-            cast(0, *c)
-        gather(stepped(grouped_ab, 0), 0, 0, 2 * G)
-        gather(stepped(grouped_cd, 0), 0, 2 * G, 4 * G)
-        for c in CASTS[1]:
-            cast(1, *c)
-        gather(late_cd[:].bitcast(U32), 1, 2 * G, 4 * G)
-        merge(grouped_cd, late_cd, 0, G)
-        merge(grouped_cd, late_cd, G, 2 * G)
-        gather(stepped(grouped_ab, 1)[:, 0:G], 1, 0, G)
-        gather(stepped(grouped_ab, 1)[:, G : 2 * G], 1, G, 2 * G)
-        quantize(grouped_ab[:, 0 : 4 * G], 0, G)
-        multiply(A, y_a, 0)
-        quantize(grouped_ab[:, 4 * G : 8 * G], G, 2 * G)
-        multiply(B, y_bcd, G)
-        quantize(grouped_cd[:], 2 * G, 4 * G)
-        multiply(C, y_bcd, G)
-        multiply(D, y_bcd, G)
-        scatter(0, y_a, 0, G)
-        scatter(1, y_bcd, G, 4 * G)
+        for i, (s0, s1) in enumerate(SCATTERS):
+            nc.vector.tensor_tensor(out_t[:].indirect(dst_t[:, s0 // 16 : s1 // 16]), y[:, s0:s1], gate_t[i][:], mult)
         nc.sync.dma_start(out, out_t[:])

@@ -13,11 +13,11 @@ FP8X4 = mybir.dt.float8_e4m3fn_x4
 FP4X4 = mybir.dt.float4_e2m1fn_x4
 
 P = 128
-VECTOR_SLOTS = (640, 640, 1024, 1024)
-CUTS = ((0, 2048, 3584, 4096), (0, 2048, 3328, 4096), (0, 2048, 3328, 4096), (0, 1792, 3328, 4096))
-SCALAR_CASTS = ((3904, 4096), (0, 0), (0, 0), (1792, 3328))
-QUANT = ((0, 1024), (1024, 2048))
-SCATTERS = ((0, 512), (512, 2048))
+G = 512
+V_END, S_END = 640, 1536
+SCATTERS = ((0, 512), (512, 1024), (1024, 1536), (1536, 2048))
+CUTS = ((0, 2560, 4096), (0, 2752, 4096), (0, 2048, 3328, 4096), (0, 2048, 3328, 4096))
+SCALAR_CASTS = ((3584, 4096), (0, 0), (0, 0), (3072, 3584))
 
 
 def tile_moe_two_lin_gelu_kernel(tc, xT, w_words, w_scales, b, gate, offs, dst, out):
@@ -32,16 +32,16 @@ def tile_moe_two_lin_gelu_kernel(tc, xT, w_words, w_scales, b, gate, offs, dst, 
         raw = [keep.tile([P, T], F32, name=f"raw{t}") for t in range(4)]
         half = [keep.tile([P, T], BF16, name=f"half{t}") for t in range(4)]
         grouped = keep.tile([P, 4 * SLOTS], BF16, name="grouped", align_bytes=64)
-        codes = keep.tile([P, SLOTS], U32, name="codes", align_bytes=64)
+        codes = keep.tile([P, S_END], U32, name="codes", align_bytes=64)
         scales = keep.tile([P, SLOTS], U8, name="scales", align_bytes=64)
         w_t = keep.tile([P, E, 2 * N], U8, name="w_t", align_bytes=64)
         ws_t = keep.tile([P, E, N], U8, name="ws_t", align_bytes=64)
         b_t = keep.tile([P, E], F32, name="b_t")
-        gate_t = [keep.tile([P, s1 - s0], F32, name=f"gate{s0}") for s0, s1 in SCATTERS]
+        gate_t = [keep.tile([P, s1 - s0], F32, name=f"gate{i}", tag=f"gate{i}", align_bytes=64) for i, (s0, s1) in enumerate(SCATTERS)]
         y = keep.tile([P, SLOTS], F32, name="y")
         out_t = keep.tile([P, T], F32, name="out_t")
         warm = keep.tile([P, 1], F32, name="warm")
-        acc = [psum.tile([P, 512], F32, name=f"acc{g}") for g in range(4)]
+        acc = [psum.tile([P, G], F32, name=f"acc{g}") for g in range(4)]
 
         x_rows = xT.rearrange("(p t) w -> p t w", t=4)
         ws_rows = w_scales.bitcast(I32).rearrange("e a q n -> (a q) e n")
@@ -60,15 +60,18 @@ def tile_moe_two_lin_gelu_kernel(tc, xT, w_words, w_scales, b, gate, offs, dst, 
                     nc.sync.dma_start(offs_t[:], offs)
         for q in range(4):
             nc.sync.dma_start(out=ws_t[32 * q : 32 * q + 4, :, :].bitcast(I32), in_=ws_rows[4 * q : 4 * q + 4, :])
-        nc.sync.dma_start(out=w_t[:].bitcast(I32), in_=w_rows)
+        nc.sync.dma_start(out=w_t[:, :4, :].bitcast(I32), in_=w_rows[:, :4, :])
         nc.sync.dma_start(b_t[:], b)
+        nc.sync.dma_start(out=w_t[:, 4:, :].bitcast(I32), in_=w_rows[:, 4:, :])
         nc.sync.dma_start(dst_t[:], dst)
         for i, (s0, s1) in enumerate(SCATTERS):
             nc.sync.dma_start(out=gate_t[i][:], in_=gate[:, s0:s1])
 
         planes = grouped[:].rearrange("p (n t) -> p t n", t=4)
+        upper_words = grouped[:].bitcast(F32).rearrange("p (n u) -> p u n", u=2)[:, 1, :]
+        parked = upper_words[:, S_END : S_END + 8]
 
-        for t in range(4):
+        def cast(t):
             lo, hi = SCALAR_CASTS[t]
             edges = sorted(set(CUTS[t]) | {lo, hi})
             for c0, c1 in zip(edges, edges[1:]):
@@ -76,28 +79,60 @@ def tile_moe_two_lin_gelu_kernel(tc, xT, w_words, w_scales, b, gate, offs, dst, 
                     nc.scalar.copy(out=half[t][:, c0:c1], in_=raw[t][:, c0:c1])
                 else:
                     nc.vector.tensor_copy(out=half[t][:, c0:c1], in_=raw[t][:, c0:c1])
-            v = VECTOR_SLOTS[t]
-            nc.vector.tensor_copy(planes[:, t, :v], raw[t][:].indirect(offs_t[:, : v // 16]))
-            nc.scalar.activation(planes[:, t, v:], half[t][:].indirect(offs_t[:, v // 16 :]), copy)
 
-        for s0, s1 in QUANT:
-            nc.vector.quantize_mx(out=codes[:, s0:s1].bitcast(FP8X4), scales=scales[:, s0:s1], in_=grouped[:, 4 * s0 : 4 * s1])
-        for g in range(4):
+        def gather_v(t, s1):
+            nc.vector.tensor_copy(planes[:, t, :s1], raw[t][:].indirect(offs_t[:, : s1 // 16]))
+
+        def gather_s(t, s0, s1):
+            nc.scalar.activation(planes[:, t, s0:s1], half[t][:].indirect(offs_t[:, s0 // 16 : s1 // 16]), copy)
+
+        def quantize(s0, s1, to):
+            nc.vector.quantize_mx(out=to.bitcast(FP8X4), scales=scales[:, s0:s1], in_=grouped[:, 4 * s0 : 4 * s1])
+
+        def multiply(g, codes):
+            biases = parked[:, 4 * g : 4 * g + 4] if 4 * g < 8 else b_t[:, 4 * g : 4 * g + 4]
             for i in range(4):
                 e = 4 * g + i
                 nc.tensor.matmul_mx(
                     out=acc[g][:, i * N : (i + 1) * N],
                     lhsT=w_t[:, e, :].bitcast(FP4X4),
                     lhsT_scale=ws_t[:, e, :],
-                    rhs=codes[:, e * N : (e + 1) * N].bitcast(FP8X4),
+                    rhs=codes[:, i * N : (i + 1) * N].bitcast(FP8X4),
                     rhs_scale=scales[:, e * N : (e + 1) * N],
                     start=True,
                     stop=True,
                 )
             for i in range(4):
                 e = 4 * g + i
-                nc.scalar.activation(out=y[:, e * N : (e + 1) * N], in_=acc[g][:, i * N : (i + 1) * N], func=gelu, bias=b_t[:, e : e + 1])
+                nc.scalar.activation(out=y[:, e * N : (e + 1) * N], in_=acc[g][:, i * N : (i + 1) * N], func=gelu, bias=biases[:, i : i + 1])
 
-        for i, (s0, s1) in enumerate(SCATTERS):
+        def scatter(i):
+            s0, s1 = SCATTERS[i]
             nc.vector.tensor_tensor(out_t[:].indirect(dst_t[:, s0 // 16 : s1 // 16]), y[:, s0:s1], gate_t[i][:], mult)
+
+        for t in (0, 1):
+            cast(t)
+            gather_v(t, 640)
+            gather_s(t, 640, SLOTS)
+        nc.scalar.copy(out=parked, in_=b_t[:, :8])
+        for t in (2, 3):
+            cast(t)
+            gather_v(t, V_END)
+            gather_s(t, V_END, S_END)
+
+        for s0, s1 in ((0, 512), (512, 1536)):
+            quantize(s0, s1, codes[:, s0:s1])
+        for g in range(2):
+            multiply(g, codes[:, g * G : (g + 1) * G])
+        for t in (2, 3):
+            gather_s(t, S_END, SLOTS)
+        multiply(2, codes[:, 2 * G : 3 * G])
+
+        for i in range(0+1):
+            scatter(i)
+        codes_last = keep.tile([P, G], U32, name="codes_last", tag="gate0", align_bytes=64)
+        quantize(S_END, SLOTS, codes_last[:])
+        multiply(3, codes_last[:])
+        for i in range(0+1, len(SCATTERS)):
+            scatter(i)
         nc.sync.dma_start(out, out_t[:])

@@ -14,10 +14,10 @@ FP4X4 = mybir.dt.float4_e2m1fn_x4
 
 P = 128
 G = 512
-V_END, S_END = 640, 1536
-SCATTERS = ((0, 512), (512, 1024), (1024, 1536), (1536, 2048))
-CUTS = ((0, 2560, 4096), (0, 2752, 4096), (0, 2048, 3328, 4096), (0, 2048, 3328, 4096))
-SCALAR_CASTS = ((3584, 4096), (0, 0), (0, 0), (3072, 3584))
+V_END, S_END = 576, 1536
+SCATTERS = ((0, 512), (512, 1024), (1024, 2048))
+CUTS = ((0, 2560, 3712, 4096), (0, 2752, 4096), (0, 2048, 3328, 4096), (0, 2048, 3328, 4096))
+SCALAR_CASTS = ((0, 0), (0, 0), (0, 0), (3072, 3584))
 
 
 def tile_moe_two_lin_gelu_kernel(tc, xT, w_words, w_scales, b, gate, offs, dst, out):
@@ -50,7 +50,7 @@ def tile_moe_two_lin_gelu_kernel(tc, xT, w_words, w_scales, b, gate, offs, dst, 
         nc.vector.memset(warm[:], 0.0)
         nc.scalar.activation(out=warm[:], in_=warm[:], func=gelu)
         nc.vector.memset(ws_t[:].rearrange("p e n -> p (e n)").bitcast(I32), 0)
-        nc.vector.memset(out_t[:], 0.0)
+        nc.gpsimd.memset(out_t[:], 0.0)
 
         for t in range(4):
             for i in range(len(CUTS[t]) - 1):
@@ -58,18 +58,19 @@ def tile_moe_two_lin_gelu_kernel(tc, xT, w_words, w_scales, b, gate, offs, dst, 
                 nc.sync.dma_start(out=raw[t][:, c0:c1], in_=x_rows[:, t, c0:c1])
                 if t == 0 and i == 0:
                     nc.sync.dma_start(offs_t[:], offs)
+        nc.sync.dma_start(b_t[:], b)
         for q in range(4):
             nc.sync.dma_start(out=ws_t[32 * q : 32 * q + 4, :, :].bitcast(I32), in_=ws_rows[4 * q : 4 * q + 4, :])
         nc.sync.dma_start(out=w_t[:, :4, :].bitcast(I32), in_=w_rows[:, :4, :])
-        nc.sync.dma_start(b_t[:], b)
-        nc.sync.dma_start(out=w_t[:, 4:, :].bitcast(I32), in_=w_rows[:, 4:, :])
         nc.sync.dma_start(dst_t[:], dst)
         for i, (s0, s1) in enumerate(SCATTERS):
             nc.sync.dma_start(out=gate_t[i][:], in_=gate[:, s0:s1])
+            if i == 0:
+                nc.sync.dma_start(out=w_t[:, 4:, :].bitcast(I32), in_=w_rows[:, 4:, :])
 
         planes = grouped[:].rearrange("p (n t) -> p t n", t=4)
         upper_words = grouped[:].bitcast(F32).rearrange("p (n u) -> p u n", u=2)[:, 1, :]
-        parked = upper_words[:, S_END : S_END + 8]
+        parked = upper_words[:, S_END : S_END + 4]
 
         def cast(t):
             lo, hi = SCALAR_CASTS[t]
@@ -90,7 +91,7 @@ def tile_moe_two_lin_gelu_kernel(tc, xT, w_words, w_scales, b, gate, offs, dst, 
             nc.vector.quantize_mx(out=to.bitcast(FP8X4), scales=scales[:, s0:s1], in_=grouped[:, 4 * s0 : 4 * s1])
 
         def multiply(g, codes):
-            biases = parked[:, 4 * g : 4 * g + 4] if 4 * g < 8 else b_t[:, 4 * g : 4 * g + 4]
+            biases = parked[:, 4 * g : 4 * g + 4] if 4 * g < 4 else b_t[:, 4 * g : 4 * g + 4]
             for i in range(4):
                 e = 4 * g + i
                 nc.tensor.matmul_mx(
@@ -112,9 +113,9 @@ def tile_moe_two_lin_gelu_kernel(tc, xT, w_words, w_scales, b, gate, offs, dst, 
 
         for t in (0, 1):
             cast(t)
-            gather_v(t, 640)
-            gather_s(t, 640, SLOTS)
-        nc.scalar.copy(out=parked, in_=b_t[:, :8])
+            gather_v(t, 672)
+            gather_s(t, 672, SLOTS)
+        nc.gpsimd.tensor_copy(out=parked, in_=b_t[:, :4])
         for t in (2, 3):
             cast(t)
             gather_v(t, V_END)
@@ -122,17 +123,16 @@ def tile_moe_two_lin_gelu_kernel(tc, xT, w_words, w_scales, b, gate, offs, dst, 
 
         for s0, s1 in ((0, 512), (512, 1536)):
             quantize(s0, s1, codes[:, s0:s1])
-        for g in range(2):
-            multiply(g, codes[:, g * G : (g + 1) * G])
+        multiply(0, codes[:, :G])
         for t in (2, 3):
             gather_s(t, S_END, SLOTS)
-        multiply(2, codes[:, 2 * G : 3 * G])
 
-        for i in range(0+1):
-            scatter(i)
-        codes_last = keep.tile([P, G], U32, name="codes_last", tag="gate0", align_bytes=64)
+        scatter(0)
+        codes_last = keep.tile([P, G], U32, name="codes_last", align_bytes=64)
         quantize(S_END, SLOTS, codes_last[:])
+        for g in range(1, 3):
+            multiply(g, codes[:, g * G : (g + 1) * G])
         multiply(3, codes_last[:])
-        for i in range(0+1, len(SCATTERS)):
+        for i in range(1, len(SCATTERS)):
             scatter(i)
         nc.sync.dma_start(out, out_t[:])

@@ -14,10 +14,10 @@ FP4X4 = mybir.dt.float4_e2m1fn_x4
 
 P = 128
 G = 512
-V_END, S_END = 576, 1536
-SCATTERS = ((0, 512), (512, 1024), (1024, 2048))
-CUTS = ((0, 2560, 3712, 4096), (0, 2752, 4096), (0, 2048, 3328, 4096), (0, 2048, 3328, 4096))
-SCALAR_CASTS = ((0, 0), (0, 0), (0, 0), (3072, 3584))
+V_LOW = 640
+HOLD = 32
+CUTS = ((0, 2560, 3712, 4096), (0, 2048, 3328, 4096), (0, 2048, 3328, 4096), (0, 2048, 3456, 4096))
+SCALAR_CASTS_LAST = (True, False, False, True)
 
 
 def tile_moe_two_lin_gelu_kernel(tc, xT, w_words, w_scales, b, gate, offs, dst, out):
@@ -32,16 +32,16 @@ def tile_moe_two_lin_gelu_kernel(tc, xT, w_words, w_scales, b, gate, offs, dst, 
         raw = [keep.tile([P, T], F32, name=f"raw{t}") for t in range(4)]
         half = [keep.tile([P, T], BF16, name=f"half{t}") for t in range(4)]
         grouped = keep.tile([P, 4 * SLOTS], BF16, name="grouped", align_bytes=64)
-        codes = keep.tile([P, S_END], U32, name="codes", align_bytes=64)
+        codes = keep.tile([P, SLOTS], U32, name="codes", align_bytes=64)
         scales = keep.tile([P, SLOTS], U8, name="scales", align_bytes=64)
         w_t = keep.tile([P, E, 2 * N], U8, name="w_t", align_bytes=64)
         ws_t = keep.tile([P, E, N], U8, name="ws_t", align_bytes=64)
         b_t = keep.tile([P, E], F32, name="b_t")
-        gate_t = [keep.tile([P, s1 - s0], F32, name=f"gate{i}", tag=f"gate{i}", align_bytes=64) for i, (s0, s1) in enumerate(SCATTERS)]
+        gate_t = keep.tile([P, SLOTS], F32, name="gate_t")
         y = keep.tile([P, SLOTS], F32, name="y")
         out_t = keep.tile([P, T], F32, name="out_t")
         warm = keep.tile([P, 1], F32, name="warm")
-        acc = [psum.tile([P, G], F32, name=f"acc{g}") for g in range(4)]
+        acc = [psum.tile([P, 2 * N], F32, name=f"acc{h}") for h in range(E // 2)]
 
         x_rows = xT.rearrange("(p t) w -> p t w", t=4)
         ws_rows = w_scales.bitcast(I32).rearrange("e a q n -> (a q) e n")
@@ -58,25 +58,24 @@ def tile_moe_two_lin_gelu_kernel(tc, xT, w_words, w_scales, b, gate, offs, dst, 
                 nc.sync.dma_start(out=raw[t][:, c0:c1], in_=x_rows[:, t, c0:c1])
                 if t == 0 and i == 0:
                     nc.sync.dma_start(offs_t[:], offs)
-        nc.sync.dma_start(b_t[:], b)
+                    nc.sync.dma_start(b_t[:], b)
         for q in range(4):
             nc.sync.dma_start(out=ws_t[32 * q : 32 * q + 4, :, :].bitcast(I32), in_=ws_rows[4 * q : 4 * q + 4, :])
-        nc.sync.dma_start(out=w_t[:, :4, :].bitcast(I32), in_=w_rows[:, :4, :])
+        nc.sync.dma_start(out=w_t[:, :8, :].bitcast(I32), in_=w_rows[:, :8, :])
         nc.sync.dma_start(dst_t[:], dst)
-        for i, (s0, s1) in enumerate(SCATTERS):
-            nc.sync.dma_start(out=gate_t[i][:], in_=gate[:, s0:s1])
-            if i == 0:
-                nc.sync.dma_start(out=w_t[:, 4:, :].bitcast(I32), in_=w_rows[:, 4:, :])
+        nc.sync.dma_start(out=gate_t[:, :G], in_=gate[:, :G])
+        nc.sync.dma_start(out=gate_t[:, G : 2 * G], in_=gate[:, G : 2 * G])
+        nc.sync.dma_start(out=w_t[:, 8:, :].bitcast(I32), in_=w_rows[:, 8:, :])
+        nc.sync.dma_start(out=gate_t[:, 2 * G :], in_=gate[:, 2 * G :])
 
         planes = grouped[:].rearrange("p (n t) -> p t n", t=4)
         upper_words = grouped[:].bitcast(F32).rearrange("p (n u) -> p u n", u=2)[:, 1, :]
-        parked = upper_words[:, S_END : S_END + 4]
+        parked = upper_words[:, 3 * G : 3 * G + 4]
 
         def cast(t):
-            lo, hi = SCALAR_CASTS[t]
-            edges = sorted(set(CUTS[t]) | {lo, hi})
-            for c0, c1 in zip(edges, edges[1:]):
-                if lo <= c0 and c1 <= hi:
+            pieces = list(zip(CUTS[t], CUTS[t][1:]))
+            for c0, c1 in pieces:
+                if SCALAR_CASTS_LAST[t] and c1 == T:
                     nc.scalar.copy(out=half[t][:, c0:c1], in_=raw[t][:, c0:c1])
                 else:
                     nc.vector.tensor_copy(out=half[t][:, c0:c1], in_=raw[t][:, c0:c1])
@@ -87,52 +86,60 @@ def tile_moe_two_lin_gelu_kernel(tc, xT, w_words, w_scales, b, gate, offs, dst, 
         def gather_s(t, s0, s1):
             nc.scalar.activation(planes[:, t, s0:s1], half[t][:].indirect(offs_t[:, s0 // 16 : s1 // 16]), copy)
 
-        def quantize(s0, s1, to):
-            nc.vector.quantize_mx(out=to.bitcast(FP8X4), scales=scales[:, s0:s1], in_=grouped[:, 4 * s0 : 4 * s1])
+        def quantize(s0, s1):
+            nc.vector.quantize_mx(out=codes[:, s0:s1].bitcast(FP8X4), scales=scales[:, s0:s1], in_=grouped[:, 4 * s0 : 4 * s1])
 
-        def multiply(g, codes):
-            biases = parked[:, 4 * g : 4 * g + 4] if 4 * g < 4 else b_t[:, 4 * g : 4 * g + 4]
-            for i in range(4):
-                e = 4 * g + i
+        def multiply(e0, e1):
+            for e in range(e0, e1):
                 nc.tensor.matmul_mx(
-                    out=acc[g][:, i * N : (i + 1) * N],
+                    out=acc[e // 2][:, (e % 2) * N : (e % 2 + 1) * N],
                     lhsT=w_t[:, e, :].bitcast(FP4X4),
                     lhsT_scale=ws_t[:, e, :],
-                    rhs=codes[:, i * N : (i + 1) * N].bitcast(FP8X4),
+                    rhs=codes[:, e * N : (e + 1) * N].bitcast(FP8X4),
                     rhs_scale=scales[:, e * N : (e + 1) * N],
                     start=True,
                     stop=True,
                 )
-            for i in range(4):
-                e = 4 * g + i
-                nc.scalar.activation(out=y[:, e * N : (e + 1) * N], in_=acc[g][:, i * N : (i + 1) * N], func=gelu, bias=biases[:, i : i + 1])
 
-        def scatter(i):
-            s0, s1 = SCATTERS[i]
-            nc.vector.tensor_tensor(out_t[:].indirect(dst_t[:, s0 // 16 : s1 // 16]), y[:, s0:s1], gate_t[i][:], mult)
+        def activate(e0, e1):
+            for e in range(e0, e1):
+                bias = parked[:, e : e + 1] if e < 4 else b_t[:, e : e + 1]
+                nc.scalar.activation(out=y[:, e * N : (e + 1) * N], in_=acc[e // 2][:, (e % 2) * N : (e % 2 + 1) * N], func=gelu, bias=bias)
 
+        def scatter(g):
+            s0, s1 = g * G, (g + 1) * G
+            nc.vector.tensor_tensor(out_t[:].indirect(dst_t[:, s0 // 16 : s1 // 16]), y[:, s0:s1], gate_t[:, s0:s1], mult)
+
+        nc.gpsimd.tensor_copy(out=parked, in_=b_t[:, :4])
         for t in (0, 1):
             cast(t)
-            gather_v(t, 672)
-            gather_s(t, 672, SLOTS)
-        nc.gpsimd.tensor_copy(out=parked, in_=b_t[:, :4])
-        for t in (2, 3):
-            cast(t)
-            gather_v(t, V_END)
-            gather_s(t, V_END, S_END)
+            gather_v(t, V_LOW)
+            gather_s(t, V_LOW, SLOTS)
+        cast(2)
+        gather_v(2, G)
+        gather_s(2, G, 3 * G)
+        cast(3)
+        gather_v(3, G)
+        gather_s(3, G, 2 * G)
 
-        for s0, s1 in ((0, 512), (512, 1536)):
-            quantize(s0, s1, codes[:, s0:s1])
-        multiply(0, codes[:, :G])
-        for t in (2, 3):
-            gather_s(t, S_END, SLOTS)
-
+        for h in (0, 1):
+            quantize(h * G // 2, (h + 1) * G // 2)
+            multiply(2 * h, 2 * h + 2)
+        quantize(G, 2 * G)
+        multiply(4, 8)
+        activate(0, 4)
+        gather_s(3, 2 * G, 3 * G + HOLD)
+        activate(4, 8)
         scatter(0)
-        codes_last = keep.tile([P, G], U32, name="codes_last", align_bytes=64)
-        quantize(S_END, SLOTS, codes_last[:])
-        for g in range(1, 3):
-            multiply(g, codes[:, g * G : (g + 1) * G])
-        multiply(3, codes_last[:])
-        for i in range(1, len(SCATTERS)):
-            scatter(i)
+        quantize(2 * G, 3 * G)
+        multiply(8, 12)
+        gather_s(2, 3 * G, SLOTS)
+        gather_s(3, 3 * G, SLOTS)
+        activate(8, 12)
+        scatter(1)
+        quantize(3 * G, SLOTS)
+        multiply(12, 16)
+        activate(12, 16)
+        scatter(2)
+        scatter(3)
         nc.sync.dma_start(out, out_t[:])

@@ -14,10 +14,16 @@ FP4X4 = mybir.dt.float4_e2m1fn_x4
 
 P = 128
 G = 512
-V_LOW = 640
+V_LOW = 768
 HOLD = 32
-CUTS = ((0, 2560, 3712, 4096), (0, 2048, 3328, 4096), (0, 2048, 3328, 4096), (0, 2048, 3456, 4096))
-SCALAR_CASTS_LAST = (True, False, False, True)
+V_PLANE2 = 832
+CUTS = ((0, 2560, 3712, 4096), (0, 1408, 3328, 4096), (0, 1408, 3328, 4096), (0, 1408, 3328, 4096))
+CASTS = (
+    ((0, 2560, "v"), (2560, 3712, "v"), (3712, 4096, "s")),
+    ((0, 1408, "g"), (1408, 3328, "v"), (3328, 4096, "v")),
+    ((0, 1408, "g"), (1408, 3328, "v"), (3328, 4096, "v")),
+    ((0, 1408, "g"), (1408, 2528, "v"), (2528, 3328, "s"), (3328, 3744, "s"), (3744, 4096, "g")),
+)
 
 
 def tile_moe_two_lin_gelu_kernel(tc, xT, w_words, w_scales, b, gate, offs, dst, out):
@@ -59,24 +65,24 @@ def tile_moe_two_lin_gelu_kernel(tc, xT, w_words, w_scales, b, gate, offs, dst, 
                 if t == 0 and i == 0:
                     nc.sync.dma_start(offs_t[:], offs)
                     nc.sync.dma_start(b_t[:], b)
-        for q in range(4):
-            nc.sync.dma_start(out=ws_t[32 * q : 32 * q + 4, :, :].bitcast(I32), in_=ws_rows[4 * q : 4 * q + 4, :])
+        for r in range(4):
+            nc.sync.dma_start(out=ws_t[r:P:32, :, :].bitcast(I32), in_=ws_rows[r:16:4, :])
         nc.sync.dma_start(out=w_t[:, :8, :].bitcast(I32), in_=w_rows[:, :8, :])
         nc.sync.dma_start(dst_t[:], dst)
         nc.sync.dma_start(out=gate_t[:, :G], in_=gate[:, :G])
-        nc.sync.dma_start(out=gate_t[:, G : 2 * G], in_=gate[:, G : 2 * G])
+        nc.sync.dma_start(out=gate_t[:, G:], in_=gate[:, G:])
         nc.sync.dma_start(out=w_t[:, 8:, :].bitcast(I32), in_=w_rows[:, 8:, :])
-        nc.sync.dma_start(out=gate_t[:, 2 * G :], in_=gate[:, 2 * G :])
 
         planes = grouped[:].rearrange("p (n t) -> p t n", t=4)
         upper_words = grouped[:].bitcast(F32).rearrange("p (n u) -> p u n", u=2)[:, 1, :]
         parked = upper_words[:, 3 * G : 3 * G + 4]
 
         def cast(t):
-            pieces = list(zip(CUTS[t], CUTS[t][1:]))
-            for c0, c1 in pieces:
-                if SCALAR_CASTS_LAST[t] and c1 == T:
+            for c0, c1, engine in CASTS[t]:
+                if engine == "s":
                     nc.scalar.copy(out=half[t][:, c0:c1], in_=raw[t][:, c0:c1])
+                elif engine == "g":
+                    nc.gpsimd.tensor_scalar(out=half[t][:, c0:c1], in0=raw[t][:, c0:c1], scalar1=1.0, scalar2=0.0, op0=mult, op1=mybir.AluOpType.add)
                 else:
                     nc.vector.tensor_copy(out=half[t][:, c0:c1], in_=raw[t][:, c0:c1])
 
@@ -116,8 +122,8 @@ def tile_moe_two_lin_gelu_kernel(tc, xT, w_words, w_scales, b, gate, offs, dst, 
             gather_v(t, V_LOW)
             gather_s(t, V_LOW, SLOTS)
         cast(2)
-        gather_v(2, G)
-        gather_s(2, G, 3 * G)
+        gather_v(2, V_PLANE2)
+        gather_s(2, V_PLANE2, 3 * G)
         cast(3)
         gather_v(3, G)
         gather_s(3, G, 2 * G)

@@ -65,17 +65,22 @@ def tile_moe_two_lin_gelu_kernel(tc, xT, w_words, w_scales, b, gate, offs, dst, 
                 if t == 0 and i == 0:
                     nc.sync.dma_start(offs_t[:], offs)
                     nc.sync.dma_start(b_t[:], b)
-        for r in range(4):
-            nc.sync.dma_start(out=ws_t[r:P:32, :, :].bitcast(I32), in_=ws_rows[r:16:4, :])
-        nc.sync.dma_start(out=w_t[:, :8, :].bitcast(I32), in_=w_rows[:, :8, :])
+        def load_scales(e0, e1):
+            for r in range(4):
+                nc.sync.dma_start(out=ws_t[r:P:32, e0:e1, :].bitcast(I32), in_=ws_rows[r:16:4, e0:e1])
+
+        load_scales(0, 4)
+        nc.sync.dma_start(out=w_t[:, :4, :].bitcast(I32), in_=w_rows[:, :4, :])
         nc.sync.dma_start(dst_t[:], dst)
         nc.sync.dma_start(out=gate_t[:, :G], in_=gate[:, :G])
-        nc.sync.dma_start(out=gate_t[:, G:], in_=gate[:, G:])
-        nc.sync.dma_start(out=w_t[:, 8:, :].bitcast(I32), in_=w_rows[:, 8:, :])
+        load_scales(4, E)
+        for g in range(1, 4):
+            nc.sync.dma_start(out=w_t[:, 4 * g : 4 * g + 4, :].bitcast(I32), in_=w_rows[:, 4 * g : 4 * g + 4, :])
+            nc.sync.dma_start(out=gate_t[:, g * G : (g + 1) * G], in_=gate[:, g * G : (g + 1) * G])
 
         planes = grouped[:].rearrange("p (n t) -> p t n", t=4)
         upper_words = grouped[:].bitcast(F32).rearrange("p (n u) -> p u n", u=2)[:, 1, :]
-        parked = upper_words[:, 3 * G : 3 * G + 4]
+        parked = {2: upper_words[:, 3 * G : 3 * G + 1], 6: upper_words[:, 3 * G + HOLD : 3 * G + HOLD + 1]}
 
         def cast(t):
             for c0, c1, engine in CASTS[t]:
@@ -109,14 +114,15 @@ def tile_moe_two_lin_gelu_kernel(tc, xT, w_words, w_scales, b, gate, offs, dst, 
 
         def activate(e0, e1):
             for e in range(e0, e1):
-                bias = parked[:, e : e + 1] if e < 4 else b_t[:, e : e + 1]
+                bias = parked.get(e, b_t[:, e : e + 1])
                 nc.scalar.activation(out=y[:, e * N : (e + 1) * N], in_=acc[e // 2][:, (e % 2) * N : (e % 2 + 1) * N], func=gelu, bias=bias)
 
         def scatter(g):
             s0, s1 = g * G, (g + 1) * G
             nc.vector.tensor_tensor(out_t[:].indirect(dst_t[:, s0 // 16 : s1 // 16]), y[:, s0:s1], gate_t[:, s0:s1], mult)
 
-        nc.gpsimd.tensor_copy(out=parked, in_=b_t[:, :4])
+        for e in (2, 6):
+            nc.gpsimd.tensor_copy(out=parked[e], in_=b_t[:, e : e + 1])
         for t in (0, 1):
             cast(t)
             gather_v(t, V_LOW)

@@ -16,13 +16,13 @@ P = 128
 G = 512
 V_LOW = 768
 HOLD = 32
-V_PLANE2 = 832
-CUTS = ((0, 2560, 3712, 4096), (0, 1408, 3328, 4096), (0, 1408, 3328, 4096), (0, 1408, 3328, 4096))
+V_PLANE2 = 768
+CUTS = ((0, 2816, 4096), (0, 1408, 3328, 4096), (0, 1408, 3328, 4096), (0, 1664, 3456, 4096))
 CASTS = (
-    ((0, 2560, "v"), (2560, 3712, "v"), (3712, 4096, "s")),
+    ((0, 2048, "v"), (2048, 2816, "s"), (2816, 3648, "v"), (3648, 4096, "s")),
     ((0, 1408, "g"), (1408, 3328, "v"), (3328, 4096, "v")),
     ((0, 1408, "g"), (1408, 3328, "v"), (3328, 4096, "v")),
-    ((0, 1408, "g"), (1408, 2528, "v"), (2528, 3328, "s"), (3328, 3744, "s"), (3744, 4096, "g")),
+    ((0, 1664, "g"), (1664, 2816, "v"), (2816, 3456, "s"), (3456, 3808, "s"), (3808, 4096, "g")),
 )
 
 
@@ -47,7 +47,9 @@ def tile_moe_two_lin_gelu_kernel(tc, xT, w_words, w_scales, b, gate, offs, dst, 
         y = keep.tile([P, SLOTS], F32, name="y")
         out_t = keep.tile([P, T], F32, name="out_t")
         warm = keep.tile([P, 1], F32, name="warm")
-        acc = [psum.tile([P, 2 * N], F32, name=f"acc{h}") for h in range(E // 2)]
+        first = [psum.tile([P, N], F32, name=f"first{e}") for e in range(4)]
+        later = [psum.tile([P, G], F32, name=f"later{g}") for g in range(3)]
+        acc = [tile[:] for tile in first] + [tile[:, i * N : (i + 1) * N] for tile in later for i in range(4)]
 
         x_rows = xT.rearrange("(p t) w -> p t w", t=4)
         ws_rows = w_scales.bitcast(I32).rearrange("e a q n -> (a q) e n")
@@ -64,11 +66,11 @@ def tile_moe_two_lin_gelu_kernel(tc, xT, w_words, w_scales, b, gate, offs, dst, 
                 nc.sync.dma_start(out=raw[t][:, c0:c1], in_=x_rows[:, t, c0:c1])
                 if t == 0 and i == 0:
                     nc.sync.dma_start(offs_t[:], offs)
-                    nc.sync.dma_start(b_t[:], b)
         def load_scales(e0, e1):
             for r in range(4):
                 nc.sync.dma_start(out=ws_t[r:P:32, e0:e1, :].bitcast(I32), in_=ws_rows[r:16:4, e0:e1])
 
+        nc.sync.dma_start(b_t[:], b)
         load_scales(0, 4)
         nc.sync.dma_start(out=w_t[:, :4, :].bitcast(I32), in_=w_rows[:, :4, :])
         nc.sync.dma_start(dst_t[:], dst)
@@ -103,7 +105,7 @@ def tile_moe_two_lin_gelu_kernel(tc, xT, w_words, w_scales, b, gate, offs, dst, 
         def multiply(e0, e1):
             for e in range(e0, e1):
                 nc.tensor.matmul_mx(
-                    out=acc[e // 2][:, (e % 2) * N : (e % 2 + 1) * N],
+                    out=acc[e],
                     lhsT=w_t[:, e, :].bitcast(FP4X4),
                     lhsT_scale=ws_t[:, e, :],
                     rhs=codes[:, e * N : (e + 1) * N].bitcast(FP8X4),
@@ -115,14 +117,12 @@ def tile_moe_two_lin_gelu_kernel(tc, xT, w_words, w_scales, b, gate, offs, dst, 
         def activate(e0, e1):
             for e in range(e0, e1):
                 bias = parked.get(e, b_t[:, e : e + 1])
-                nc.scalar.activation(out=y[:, e * N : (e + 1) * N], in_=acc[e // 2][:, (e % 2) * N : (e % 2 + 1) * N], func=gelu, bias=bias)
+                nc.scalar.activation(out=y[:, e * N : (e + 1) * N], in_=acc[e], func=gelu, bias=bias)
 
         def scatter(g):
             s0, s1 = g * G, (g + 1) * G
             nc.vector.tensor_tensor(out_t[:].indirect(dst_t[:, s0 // 16 : s1 // 16]), y[:, s0:s1], gate_t[:, s0:s1], mult)
 
-        for e in (2, 6):
-            nc.gpsimd.tensor_copy(out=parked[e], in_=b_t[:, e : e + 1])
         for t in (0, 1):
             cast(t)
             gather_v(t, V_LOW)
@@ -133,10 +133,12 @@ def tile_moe_two_lin_gelu_kernel(tc, xT, w_words, w_scales, b, gate, offs, dst, 
         cast(3)
         gather_v(3, G)
         gather_s(3, G, 2 * G)
+        for e in (2, 6):
+            nc.gpsimd.tensor_copy(out=parked[e], in_=b_t[:, e : e + 1])
 
-        for h in (0, 1):
-            quantize(h * G // 2, (h + 1) * G // 2)
-            multiply(2 * h, 2 * h + 2)
+        for e in range(4):
+            quantize(e * N, (e + 1) * N)
+            multiply(e, e + 1)
         quantize(G, 2 * G)
         multiply(4, 8)
         activate(0, 4)

@@ -16,13 +16,13 @@ P = 128
 G = 512
 V_LOW = 768
 HOLD = 32
-V_PLANE2 = 768
-CUTS = ((0, 2816, 4096), (0, 1408, 3328, 4096), (0, 1408, 3328, 4096), (0, 1664, 3456, 4096))
+V_PLANE2 = 640
+CUTS = ((0, 2816, 4096), (0, 1280, 3328, 4096), (0, 1280, 3328, 4096), (0, 1280, 2816, 3584, 4096))
 CASTS = (
     ((0, 2048, "v"), (2048, 2816, "s"), (2816, 3648, "v"), (3648, 4096, "s")),
-    ((0, 1408, "g"), (1408, 3328, "v"), (3328, 4096, "v")),
-    ((0, 1408, "g"), (1408, 3328, "v"), (3328, 4096, "v")),
-    ((0, 1664, "g"), (1664, 2816, "v"), (2816, 3456, "s"), (3456, 3808, "s"), (3808, 4096, "g")),
+    ((0, 1280, "g"), (1280, 3328, "v"), (3328, 4096, "v")),
+    ((0, 1280, "g"), (1280, 3328, "v"), (3328, 4096, "v")),
+    ((0, 1280, "g"), (1280, 2816, "v"), (2816, 3584, "v"), (3584, 3872, "s"), (3872, 4096, "g")),
 )
 
 

@@ -14,16 +14,18 @@ FP4X4 = mybir.dt.float4_e2m1fn_x4
 
 P = 128
 G = 512
-V_LOW = 768
-HOLD = 32
-V_PLANE2 = 640
-CUTS = ((0, 2816, 4096), (0, 1280, 3328, 4096), (0, 1280, 3328, 4096), (0, 1280, 2816, 3584, 4096))
-CASTS = (
-    ((0, 2048, "v"), (2048, 2816, "s"), (2816, 3648, "v"), (3648, 4096, "s")),
-    ((0, 1280, "g"), (1280, 3328, "v"), (3328, 4096, "v")),
-    ((0, 1280, "g"), (1280, 3328, "v"), (3328, 4096, "v")),
-    ((0, 1280, "g"), (1280, 2816, "v"), (2816, 3584, "v"), (3584, 3872, "s"), (3872, 4096, "g")),
+EG = G // N
+
+VECTOR_SLOTS = (1024, 704, 640, G)
+
+LOADS = (
+    ((("vector", 2048), ("scalar", 2816)), (("vector", 3648), ("scalar", T))),
+    ((("gpsimd", 1792),), (("vector", 3328), ("scalar", T))),
+    ((("gpsimd", 1280),), (("vector", 3328),), (("vector", T),)),
+    ((("gpsimd", 1280),), (("vector", 2816),), (("vector", 3584),), (("scalar", 3872), ("gpsimd", T))),
 )
+
+LIST_STEP = 32
 
 
 def tile_moe_two_lin_gelu_kernel(tc, xT, w_words, w_scales, b, gate, offs, dst, out):
@@ -31,6 +33,7 @@ def tile_moe_two_lin_gelu_kernel(tc, xT, w_words, w_scales, b, gate, offs, dst, 
     gelu = mybir.ActivationFunctionType.Gelu_apprx_tanh
     copy = mybir.ActivationFunctionType.Copy
     mult = mybir.AluOpType.mult
+    add = mybir.AluOpType.add
 
     with tc.tile_pool(name="keep", bufs=1) as keep, tc.psum_pool(name="psum", bufs=1) as psum:
         offs_t = keep.tile([P, SLOTS // 16], U16, name="offs_t")
@@ -47,9 +50,9 @@ def tile_moe_two_lin_gelu_kernel(tc, xT, w_words, w_scales, b, gate, offs, dst, 
         y = keep.tile([P, SLOTS], F32, name="y")
         out_t = keep.tile([P, T], F32, name="out_t")
         warm = keep.tile([P, 1], F32, name="warm")
-        first = [psum.tile([P, N], F32, name=f"first{e}") for e in range(4)]
+        first = [psum.tile([P, N], F32, name=f"first{e}") for e in range(EG)]
         later = [psum.tile([P, G], F32, name=f"later{g}") for g in range(3)]
-        acc = [tile[:] for tile in first] + [tile[:, i * N : (i + 1) * N] for tile in later for i in range(4)]
+        acc = [tile[:] for tile in first] + [tile[:, i * N : (i + 1) * N] for tile in later for i in range(EG)]
 
         x_rows = xT.rearrange("(p t) w -> p t w", t=4)
         ws_rows = w_scales.bitcast(I32).rearrange("e a q n -> (a q) e n")
@@ -61,42 +64,56 @@ def tile_moe_two_lin_gelu_kernel(tc, xT, w_words, w_scales, b, gate, offs, dst, 
         nc.gpsimd.memset(out_t[:], 0.0)
 
         for t in range(4):
-            for i in range(len(CUTS[t]) - 1):
-                c0, c1 = CUTS[t][i : i + 2]
+            c0 = 0
+            for shares in LOADS[t]:
+                c1 = shares[-1][1]
                 nc.sync.dma_start(out=raw[t][:, c0:c1], in_=x_rows[:, t, c0:c1])
-                if t == 0 and i == 0:
+                if t == 0 and c0 == 0:
                     nc.sync.dma_start(offs_t[:], offs)
+                c0 = c1
+
         def load_scales(e0, e1):
             for r in range(4):
                 nc.sync.dma_start(out=ws_t[r:P:32, e0:e1, :].bitcast(I32), in_=ws_rows[r:16:4, e0:e1])
 
-        nc.sync.dma_start(b_t[:], b)
-        load_scales(0, 4)
-        nc.sync.dma_start(out=w_t[:, :4, :].bitcast(I32), in_=w_rows[:, :4, :])
-        nc.sync.dma_start(dst_t[:], dst)
-        nc.sync.dma_start(out=gate_t[:, :G], in_=gate[:, :G])
-        load_scales(4, E)
-        for g in range(1, 4):
-            nc.sync.dma_start(out=w_t[:, 4 * g : 4 * g + 4, :].bitcast(I32), in_=w_rows[:, 4 * g : 4 * g + 4, :])
+        def load_weights(g):
+            nc.sync.dma_start(out=w_t[:, EG * g : EG * g + EG, :].bitcast(I32), in_=w_rows[:, EG * g : EG * g + EG, :])
+
+        def load_gate(g):
             nc.sync.dma_start(out=gate_t[:, g * G : (g + 1) * G], in_=gate[:, g * G : (g + 1) * G])
 
+        nc.sync.dma_start(b_t[:], b)
+        load_scales(0, EG)
+        for e in (0, 2):
+            nc.sync.dma_start(out=w_t[:, e : e + 2, :].bitcast(I32), in_=w_rows[:, e : e + 2, :])
+        nc.sync.dma_start(dst_t[:], dst)
+        load_gate(0)
+        load_scales(EG, E)
+        for g in range(1, 4):
+            load_weights(g)
+            load_gate(g)
+
         planes = grouped[:].rearrange("p (n t) -> p t n", t=4)
+
         upper_words = grouped[:].bitcast(F32).rearrange("p (n u) -> p u n", u=2)[:, 1, :]
-        parked = {2: upper_words[:, 3 * G : 3 * G + 1], 6: upper_words[:, 3 * G + HOLD : 3 * G + HOLD + 1]}
+        parked = {EG * g + 2: upper_words[:, 3 * G + g * LIST_STEP : 3 * G + g * LIST_STEP + 1] for g in (0, 1)}
 
-        def cast(t):
-            for c0, c1, engine in CASTS[t]:
-                if engine == "s":
-                    nc.scalar.copy(out=half[t][:, c0:c1], in_=raw[t][:, c0:c1])
-                elif engine == "g":
-                    nc.gpsimd.tensor_scalar(out=half[t][:, c0:c1], in0=raw[t][:, c0:c1], scalar1=1.0, scalar2=0.0, op0=mult, op1=mybir.AluOpType.add)
-                else:
-                    nc.vector.tensor_copy(out=half[t][:, c0:c1], in_=raw[t][:, c0:c1])
+        def round_plane(t):
+            c0 = 0
+            for shares in LOADS[t]:
+                for engine, c1 in shares:
+                    if engine == "scalar":
+                        nc.scalar.copy(out=half[t][:, c0:c1], in_=raw[t][:, c0:c1])
+                    elif engine == "gpsimd":
+                        nc.gpsimd.tensor_scalar(out=half[t][:, c0:c1], in0=raw[t][:, c0:c1], scalar1=1.0, scalar2=0.0, op0=mult, op1=add)
+                    else:
+                        nc.vector.tensor_copy(out=half[t][:, c0:c1], in_=raw[t][:, c0:c1])
+                    c0 = c1
 
-        def gather_v(t, s1):
+        def gather_vector(t, s1):
             nc.vector.tensor_copy(planes[:, t, :s1], raw[t][:].indirect(offs_t[:, : s1 // 16]))
 
-        def gather_s(t, s0, s1):
+        def gather_scalar(t, s0, s1):
             nc.scalar.activation(planes[:, t, s0:s1], half[t][:].indirect(offs_t[:, s0 // 16 : s1 // 16]), copy)
 
         def quantize(s0, s1):
@@ -114,8 +131,12 @@ def tile_moe_two_lin_gelu_kernel(tc, xT, w_words, w_scales, b, gate, offs, dst, 
                     stop=True,
                 )
 
-        def activate(e0, e1):
-            for e in range(e0, e1):
+        def quantize_and_multiply(g):
+            quantize(g * G, (g + 1) * G)
+            multiply(EG * g, EG * g + EG)
+
+        def activate(g):
+            for e in range(EG * g, EG * g + EG):
                 bias = parked.get(e, b_t[:, e : e + 1])
                 nc.scalar.activation(out=y[:, e * N : (e + 1) * N], in_=acc[e], func=gelu, bias=bias)
 
@@ -123,37 +144,29 @@ def tile_moe_two_lin_gelu_kernel(tc, xT, w_words, w_scales, b, gate, offs, dst, 
             s0, s1 = g * G, (g + 1) * G
             nc.vector.tensor_tensor(out_t[:].indirect(dst_t[:, s0 // 16 : s1 // 16]), y[:, s0:s1], gate_t[:, s0:s1], mult)
 
-        for t in (0, 1):
-            cast(t)
-            gather_v(t, V_LOW)
-            gather_s(t, V_LOW, SLOTS)
-        cast(2)
-        gather_v(2, V_PLANE2)
-        gather_s(2, V_PLANE2, 3 * G)
-        cast(3)
-        gather_v(3, G)
-        gather_s(3, G, 2 * G)
-        for e in (2, 6):
+        for t, s1 in enumerate((SLOTS, SLOTS, 3 * G, 2 * G)):
+            round_plane(t)
+            gather_vector(t, VECTOR_SLOTS[t])
+            gather_scalar(t, VECTOR_SLOTS[t], s1)
+        for e in sorted(parked):
             nc.gpsimd.tensor_copy(out=parked[e], in_=b_t[:, e : e + 1])
 
-        for e in range(4):
+        for e in range(EG):
             quantize(e * N, (e + 1) * N)
             multiply(e, e + 1)
-        quantize(G, 2 * G)
-        multiply(4, 8)
-        activate(0, 4)
-        gather_s(3, 2 * G, 3 * G + HOLD)
-        activate(4, 8)
+        quantize_and_multiply(1)
+        activate(0)
+        gather_scalar(3, 2 * G, 3 * G + LIST_STEP)
+        activate(1)
+
         scatter(0)
-        quantize(2 * G, 3 * G)
-        multiply(8, 12)
-        gather_s(2, 3 * G, SLOTS)
-        gather_s(3, 3 * G, SLOTS)
-        activate(8, 12)
+        quantize_and_multiply(2)
+        gather_scalar(2, 3 * G, SLOTS)
+        gather_scalar(3, 3 * G, SLOTS)
+        activate(2)
         scatter(1)
-        quantize(3 * G, SLOTS)
-        multiply(12, 16)
-        activate(12, 16)
+        quantize_and_multiply(3)
+        activate(3)
         scatter(2)
         scatter(3)
         nc.sync.dma_start(out, out_t[:])

@@ -16,12 +16,12 @@ P = 128
 G = 512
 EG = G // N
 
-VECTOR_SLOTS = (1024, 704, 640, G)
+VECTOR_SLOTS = (1344, 1344, 640, G)
 
 LOADS = (
-    ((("vector", 2048), ("scalar", 2816)), (("vector", 3648), ("scalar", T))),
+    ((("gpsimd", 1920), ("scalar", T)),),
+    ((("gpsimd", 1792),), (("gpsimd", 3040), ("scalar", T))),
     ((("gpsimd", 1792),), (("vector", 3328), ("scalar", T))),
-    ((("gpsimd", 1280),), (("vector", 3328),), (("vector", T),)),
     ((("gpsimd", 1280),), (("vector", 2816),), (("vector", 3584),), (("scalar", 3872), ("gpsimd", T))),
 )
 
@@ -61,7 +61,7 @@ def tile_moe_two_lin_gelu_kernel(tc, xT, w_words, w_scales, b, gate, offs, dst, 
         nc.vector.memset(warm[:], 0.0)
         nc.scalar.activation(out=warm[:], in_=warm[:], func=gelu)
         nc.vector.memset(ws_t[:].rearrange("p e n -> p (e n)").bitcast(I32), 0)
-        nc.gpsimd.memset(out_t[:], 0.0)
+        nc.vector.memset(out_t[:], 0.0)
 
         for t in range(4):
             c0 = 0
@@ -76,22 +76,22 @@ def tile_moe_two_lin_gelu_kernel(tc, xT, w_words, w_scales, b, gate, offs, dst, 
             for r in range(4):
                 nc.sync.dma_start(out=ws_t[r:P:32, e0:e1, :].bitcast(I32), in_=ws_rows[r:16:4, e0:e1])
 
-        def load_weights(g):
-            nc.sync.dma_start(out=w_t[:, EG * g : EG * g + EG, :].bitcast(I32), in_=w_rows[:, EG * g : EG * g + EG, :])
+        def load_weights(e0, e1):
+            nc.sync.dma_start(out=w_t[:, e0:e1, :].bitcast(I32), in_=w_rows[:, e0:e1, :])
 
-        def load_gate(g):
-            nc.sync.dma_start(out=gate_t[:, g * G : (g + 1) * G], in_=gate[:, g * G : (g + 1) * G])
+        def load_gate(e0, e1):
+            nc.sync.dma_start(out=gate_t[:, e0 * N : e1 * N], in_=gate[:, e0 * N : e1 * N])
 
         nc.sync.dma_start(b_t[:], b)
         load_scales(0, EG)
-        for e in (0, 2):
-            nc.sync.dma_start(out=w_t[:, e : e + 2, :].bitcast(I32), in_=w_rows[:, e : e + 2, :])
+        load_weights(0, 2)
+        load_weights(2, EG)
         nc.sync.dma_start(dst_t[:], dst)
-        load_gate(0)
-        load_scales(EG, E)
-        for g in range(1, 4):
-            load_weights(g)
-            load_gate(g)
+        load_gate(0, EG)
+        for e0, e1 in ((EG, 2 * EG), (2 * EG, E)):
+            load_scales(e0, e1)
+            load_weights(e0, e1)
+            load_gate(e0, e1)
 
         planes = grouped[:].rearrange("p (n t) -> p t n", t=4)
 

@@ -16,16 +16,17 @@ P = 128
 G = 512
 EG = G // N
 
-VECTOR_SLOTS = (1344, 1344, 640, G)
+FIRST, SECOND, THIRD, LAST = 0, 3 * G, 2 * G, G
 
 LOADS = (
     ((("gpsimd", 1920), ("scalar", T)),),
-    ((("gpsimd", 1792),), (("gpsimd", 3040), ("scalar", T))),
-    ((("gpsimd", 1792),), (("vector", 3328), ("scalar", T))),
-    ((("gpsimd", 1280),), (("vector", 2816),), (("vector", 3584),), (("scalar", 3872), ("gpsimd", T))),
+    ((("gpsimd", 1920), ("scalar", T)),),
+    ((("gpsimd", 1600),), (("gpsimd", 2784), ("scalar", T))),
+    ((("gpsimd", 1152),), (("vector", 2816),), (("vector", 3328), ("scalar", 3584)), (("scalar", 3872), ("gpsimd", T))),
 )
 
 LIST_STEP = 32
+WEAVE_AHEAD = 3
 
 
 def tile_moe_two_lin_gelu_kernel(tc, xT, w_words, w_scales, b, gate, offs, dst, out):
@@ -41,6 +42,7 @@ def tile_moe_two_lin_gelu_kernel(tc, xT, w_words, w_scales, b, gate, offs, dst, 
         raw = [keep.tile([P, T], F32, name=f"raw{t}") for t in range(4)]
         half = [keep.tile([P, T], BF16, name=f"half{t}") for t in range(4)]
         grouped = keep.tile([P, 4 * SLOTS], BF16, name="grouped", align_bytes=64)
+        pairs = keep.tile([P, 4 * 2 * G], BF16, name="pairs", align_bytes=64)
         codes = keep.tile([P, SLOTS], U32, name="codes", align_bytes=64)
         scales = keep.tile([P, SLOTS], U8, name="scales", align_bytes=64)
         w_t = keep.tile([P, E, 2 * N], U8, name="w_t", align_bytes=64)
@@ -72,31 +74,43 @@ def tile_moe_two_lin_gelu_kernel(tc, xT, w_words, w_scales, b, gate, offs, dst, 
                     nc.sync.dma_start(offs_t[:], offs)
                 c0 = c1
 
-        def load_scales(e0, e1):
+        def load_scales(s0, s1):
             for r in range(4):
-                nc.sync.dma_start(out=ws_t[r:P:32, e0:e1, :].bitcast(I32), in_=ws_rows[r:16:4, e0:e1])
+                nc.sync.dma_start(out=ws_t[r:P:32, s0 // N : s1 // N, :].bitcast(I32), in_=ws_rows[r:16:4, s0 // N : s1 // N])
 
-        def load_weights(e0, e1):
-            nc.sync.dma_start(out=w_t[:, e0:e1, :].bitcast(I32), in_=w_rows[:, e0:e1, :])
+        def load_weights(s0, s1):
+            nc.sync.dma_start(out=w_t[:, s0 // N : s1 // N, :].bitcast(I32), in_=w_rows[:, s0 // N : s1 // N, :])
 
-        def load_gate(e0, e1):
-            nc.sync.dma_start(out=gate_t[:, e0 * N : e1 * N], in_=gate[:, e0 * N : e1 * N])
+        def load_gate(s0, s1):
+            nc.sync.dma_start(out=gate_t[:, s0:s1], in_=gate[:, s0:s1])
 
         nc.sync.dma_start(b_t[:], b)
-        load_scales(0, EG)
-        load_weights(0, 2)
-        load_weights(2, EG)
+        load_scales(FIRST, FIRST + G)
+        load_weights(FIRST, FIRST + 2 * N)
+        load_weights(FIRST + 2 * N, FIRST + G)
         nc.sync.dma_start(dst_t[:], dst)
-        load_gate(0, EG)
-        for e0, e1 in ((EG, 2 * EG), (2 * EG, E)):
-            load_scales(e0, e1)
-            load_weights(e0, e1)
-            load_gate(e0, e1)
+        load_gate(FIRST, FIRST + G)
+        load_scales(SECOND, SECOND + G)
+        load_weights(SECOND, SECOND + G)
+        load_gate(SECOND, SECOND + G)
+        load_scales(LAST, THIRD + G)
+        load_weights(THIRD, THIRD + G)
+        load_weights(LAST, LAST + G)
+        load_gate(LAST, THIRD + G)
 
         planes = grouped[:].rearrange("p (n t) -> p t n", t=4)
+        pair_planes = pairs[:].rearrange("p (u n v) -> p u v n", u=2, v=2)
+
+        def place(t, s0, s1):
+            if s1 <= 2 * G:
+                return pair_planes[:, t // 2, t % 2, s0:s1]
+            return planes[:, t, s0:s1]
 
         upper_words = grouped[:].bitcast(F32).rearrange("p (n u) -> p u n", u=2)[:, 1, :]
-        parked = {EG * g + 2: upper_words[:, 3 * G + g * LIST_STEP : 3 * G + g * LIST_STEP + 1] for g in (0, 1)}
+        parked = {
+            FIRST // N + 2: upper_words[:, THIRD - 1 : THIRD],
+            SECOND // N + 2: pairs[:].bitcast(F32)[:, 2 * G + LAST : 2 * G + LAST + 1],
+        }
 
         def round_plane(t):
             c0 = 0
@@ -110,17 +124,23 @@ def tile_moe_two_lin_gelu_kernel(tc, xT, w_words, w_scales, b, gate, offs, dst, 
                         nc.vector.tensor_copy(out=half[t][:, c0:c1], in_=raw[t][:, c0:c1])
                     c0 = c1
 
-        def gather_vector(t, s1):
-            nc.vector.tensor_copy(planes[:, t, :s1], raw[t][:].indirect(offs_t[:, : s1 // 16]))
+        def gather_vector(t, s0, s1):
+            nc.vector.tensor_copy(place(t, s0, s1), raw[t][:].indirect(offs_t[:, s0 // 16 : s1 // 16]))
 
         def gather_scalar(t, s0, s1):
-            nc.scalar.activation(planes[:, t, s0:s1], half[t][:].indirect(offs_t[:, s0 // 16 : s1 // 16]), copy)
+            nc.scalar.activation(place(t, s0, s1), half[t][:].indirect(offs_t[:, s0 // 16 : s1 // 16]), copy)
+
+        def weave(move, dtype, s0, s1):
+            move(
+                out=grouped[:].bitcast(dtype).rearrange("p (n u) -> p n u", u=2)[:, s0:s1, :],
+                in_=pairs[:].bitcast(dtype).rearrange("p (u n) -> p n u", u=2)[:, s0:s1, :],
+            )
 
         def quantize(s0, s1):
             nc.vector.quantize_mx(out=codes[:, s0:s1].bitcast(FP8X4), scales=scales[:, s0:s1], in_=grouped[:, 4 * s0 : 4 * s1])
 
-        def multiply(e0, e1):
-            for e in range(e0, e1):
+        def multiply(s0, s1):
+            for e in range(s0 // N, s1 // N):
                 nc.tensor.matmul_mx(
                     out=acc[e],
                     lhsT=w_t[:, e, :].bitcast(FP4X4),
@@ -131,42 +151,53 @@ def tile_moe_two_lin_gelu_kernel(tc, xT, w_words, w_scales, b, gate, offs, dst, 
                     stop=True,
                 )
 
-        def quantize_and_multiply(g):
-            quantize(g * G, (g + 1) * G)
-            multiply(EG * g, EG * g + EG)
+        def quantize_and_multiply(s0, s1):
+            quantize(s0, s1)
+            multiply(s0, s1)
 
-        def activate(g):
-            for e in range(EG * g, EG * g + EG):
+        def activate(s0):
+            for e in range(s0 // N, s0 // N + EG):
                 bias = parked.get(e, b_t[:, e : e + 1])
                 nc.scalar.activation(out=y[:, e * N : (e + 1) * N], in_=acc[e], func=gelu, bias=bias)
 
-        def scatter(g):
-            s0, s1 = g * G, (g + 1) * G
+        def scatter(s0):
+            s1 = s0 + G
             nc.vector.tensor_tensor(out_t[:].indirect(dst_t[:, s0 // 16 : s1 // 16]), y[:, s0:s1], gate_t[:, s0:s1], mult)
 
-        for t, s1 in enumerate((SLOTS, SLOTS, 3 * G, 2 * G)):
+        for t in (0, 1):
             round_plane(t)
-            gather_vector(t, VECTOR_SLOTS[t])
-            gather_scalar(t, VECTOR_SLOTS[t], s1)
+            gather_vector(t, FIRST, LAST + G)
+            gather_vector(t, SECOND, SECOND + G)
+            gather_scalar(t, THIRD, THIRD + G)
+        round_plane(2)
+        gather_vector(2, FIRST, FIRST + G)
+        gather_vector(2, SECOND, SECOND + G)
+        gather_scalar(2, THIRD, THIRD + G)
+        round_plane(3)
+        gather_vector(3, FIRST, FIRST + G)
+        gather_scalar(3, SECOND, SECOND + G)
         for e in sorted(parked):
             nc.gpsimd.tensor_copy(out=parked[e], in_=b_t[:, e : e + 1])
 
-        for e in range(EG):
-            quantize(e * N, (e + 1) * N)
-            multiply(e, e + 1)
-        quantize_and_multiply(1)
-        activate(0)
-        gather_scalar(3, 2 * G, 3 * G + LIST_STEP)
-        activate(1)
+        for e in range(EG + WEAVE_AHEAD):
+            if e >= WEAVE_AHEAD:
+                quantize_and_multiply((e - WEAVE_AHEAD) * N, (e - WEAVE_AHEAD + 1) * N)
+            if e < EG:
+                weave(nc.vector.tensor_copy, I32, e * N, (e + 1) * N)
+        quantize_and_multiply(SECOND, SECOND + G)
+        activate(FIRST)
+        gather_scalar(3, THIRD - LIST_STEP, THIRD + G)
+        activate(SECOND)
 
-        scatter(0)
-        quantize_and_multiply(2)
-        gather_scalar(2, 3 * G, SLOTS)
-        gather_scalar(3, 3 * G, SLOTS)
-        activate(2)
-        scatter(1)
-        quantize_and_multiply(3)
-        activate(3)
-        scatter(2)
-        scatter(3)
+        scatter(FIRST)
+        quantize_and_multiply(THIRD, THIRD + G)
+        gather_scalar(2, LAST, LAST + G)
+        gather_scalar(3, LAST, LAST + G)
+        weave(nc.scalar.copy, U32, LAST, LAST + G)
+        activate(THIRD)
+        scatter(SECOND)
+        quantize_and_multiply(LAST, LAST + G)
+        activate(LAST)
+        scatter(THIRD)
+        scatter(LAST)
         nc.sync.dma_start(out, out_t[:])

@@ -16,13 +16,13 @@ P = 128
 G = 512
 EG = G // N
 
-FIRST, SECOND, THIRD, LAST = 0, 3 * G, 2 * G, G
+FIRST, SECOND, THIRD, LAST = 0, G, 2 * G, 3 * G
 
 LOADS = (
     ((("gpsimd", 1920), ("scalar", T)),),
     ((("gpsimd", 1920), ("scalar", T)),),
-    ((("gpsimd", 1600),), (("gpsimd", 2784), ("scalar", T))),
-    ((("gpsimd", 1152),), (("vector", 2816),), (("vector", 3328), ("scalar", 3584)), (("scalar", 3872), ("gpsimd", T))),
+    ((("gpsimd", 1920), ("scalar", T)),),
+    ((("gpsimd", 1088), ("scalar", 2304)), (("vector", 3072), ("scalar", 3584)), (("scalar", 3872), ("gpsimd", T))),
 )
 
 LIST_STEP = 32
@@ -91,12 +91,13 @@ def tile_moe_two_lin_gelu_kernel(tc, xT, w_words, w_scales, b, gate, offs, dst, 
         nc.sync.dma_start(dst_t[:], dst)
         load_gate(FIRST, FIRST + G)
         load_scales(SECOND, SECOND + G)
-        load_weights(SECOND, SECOND + G)
+        load_weights(SECOND, SECOND + 2 * N)
+        load_weights(SECOND + 2 * N, SECOND + G)
         load_gate(SECOND, SECOND + G)
-        load_scales(LAST, THIRD + G)
-        load_weights(THIRD, THIRD + G)
-        load_weights(LAST, LAST + G)
-        load_gate(LAST, THIRD + G)
+        load_scales(THIRD, SLOTS)
+        for s0 in (THIRD, LAST):
+            load_weights(s0, s0 + G)
+            load_gate(s0, s0 + G)
 
         planes = grouped[:].rearrange("p (n t) -> p t n", t=4)
         pair_planes = pairs[:].rearrange("p (u n v) -> p u v n", u=2, v=2)
@@ -107,10 +108,7 @@ def tile_moe_two_lin_gelu_kernel(tc, xT, w_words, w_scales, b, gate, offs, dst, 
             return planes[:, t, s0:s1]
 
         upper_words = grouped[:].bitcast(F32).rearrange("p (n u) -> p u n", u=2)[:, 1, :]
-        parked = {
-            FIRST // N + 2: upper_words[:, THIRD - 1 : THIRD],
-            SECOND // N + 2: pairs[:].bitcast(F32)[:, 2 * G + LAST : 2 * G + LAST + 1],
-        }
+        parked = {EG * g + 2: upper_words[:, LAST + g * LIST_STEP : LAST + g * LIST_STEP + 1] for g in (0, 1)}
 
         def round_plane(t):
             c0 = 0
@@ -166,13 +164,12 @@ def tile_moe_two_lin_gelu_kernel(tc, xT, w_words, w_scales, b, gate, offs, dst, 
 
         for t in (0, 1):
             round_plane(t)
-            gather_vector(t, FIRST, LAST + G)
-            gather_vector(t, SECOND, SECOND + G)
-            gather_scalar(t, THIRD, THIRD + G)
+            gather_vector(t, FIRST, THIRD)
+            gather_vector(t, THIRD, LAST)
+            gather_scalar(t, LAST, SLOTS)
         round_plane(2)
-        gather_vector(2, FIRST, FIRST + G)
-        gather_vector(2, SECOND, SECOND + G)
-        gather_scalar(2, THIRD, THIRD + G)
+        gather_vector(2, FIRST, THIRD)
+        gather_vector(2, THIRD, LAST)
         round_plane(3)
         gather_vector(3, FIRST, FIRST + G)
         gather_scalar(3, SECOND, SECOND + G)
@@ -184,16 +181,18 @@ def tile_moe_two_lin_gelu_kernel(tc, xT, w_words, w_scales, b, gate, offs, dst, 
                 quantize_and_multiply((e - WEAVE_AHEAD) * N, (e - WEAVE_AHEAD + 1) * N)
             if e < EG:
                 weave(nc.vector.tensor_copy, I32, e * N, (e + 1) * N)
-        quantize_and_multiply(SECOND, SECOND + G)
+        weave(nc.scalar.copy, U32, SECOND, SECOND + G // 2)
+        weave(nc.vector.tensor_copy, I32, SECOND + G // 2, SECOND + G)
+        quantize_and_multiply(SECOND, SECOND + G // 2)
+        quantize_and_multiply(SECOND + G // 2, SECOND + G)
         activate(FIRST)
-        gather_scalar(3, THIRD - LIST_STEP, THIRD + G)
+        gather_scalar(3, THIRD, THIRD + G + LIST_STEP)
         activate(SECOND)
 
         scatter(FIRST)
         quantize_and_multiply(THIRD, THIRD + G)
         gather_scalar(2, LAST, LAST + G)
         gather_scalar(3, LAST, LAST + G)
-        weave(nc.scalar.copy, U32, LAST, LAST + G)
         activate(THIRD)
         scatter(SECOND)
         quantize_and_multiply(LAST, LAST + G)

@@ -16,7 +16,7 @@ P = 128
 G = 512
 EG = G // N
 
-FIRST, SECOND, THIRD, LAST = 0, G, 2 * G, 3 * G
+FIRST, SECOND, THIRD, LAST = G, 2 * G, 0, 3 * G
 
 LOADS = (
     ((("gpsimd", 1920), ("scalar", T)),),
@@ -52,9 +52,15 @@ def tile_moe_two_lin_gelu_kernel(tc, xT, w_words, w_scales, b, gate, offs, dst, 
         y = keep.tile([P, SLOTS], F32, name="y")
         out_t = keep.tile([P, T], F32, name="out_t")
         warm = keep.tile([P, 1], F32, name="warm")
-        first = [psum.tile([P, N], F32, name=f"first{e}") for e in range(EG)]
-        later = [psum.tile([P, G], F32, name=f"later{g}") for g in range(3)]
-        acc = [tile[:] for tile in first] + [tile[:, i * N : (i + 1) * N] for tile in later for i in range(EG)]
+        acc = {}
+        for s0 in (FIRST, SECOND, THIRD, LAST):
+            if s0 == FIRST:
+                parts = [psum.tile([P, N], F32, name=f"first{i}")[:] for i in range(EG)]
+            else:
+                bank = psum.tile([P, G], F32, name=f"bank{s0}")
+                parts = [bank[:, i * N : (i + 1) * N] for i in range(EG)]
+            for i in range(EG):
+                acc[s0 // N + i] = parts[i]
 
         x_rows = xT.rearrange("(p t) w -> p t w", t=4)
         ws_rows = w_scales.bitcast(I32).rearrange("e a q n -> (a q) e n")
@@ -90,11 +96,11 @@ def tile_moe_two_lin_gelu_kernel(tc, xT, w_words, w_scales, b, gate, offs, dst, 
         load_weights(FIRST + 2 * N, FIRST + G)
         nc.sync.dma_start(dst_t[:], dst)
         load_gate(FIRST, FIRST + G)
-        load_scales(SECOND, SECOND + G)
+        load_scales(SECOND, SLOTS)
         load_weights(SECOND, SECOND + 2 * N)
         load_weights(SECOND + 2 * N, SECOND + G)
         load_gate(SECOND, SECOND + G)
-        load_scales(THIRD, SLOTS)
+        load_scales(THIRD, THIRD + G)
         for s0 in (THIRD, LAST):
             load_weights(s0, s0 + G)
             load_gate(s0, s0 + G)
@@ -108,7 +114,11 @@ def tile_moe_two_lin_gelu_kernel(tc, xT, w_words, w_scales, b, gate, offs, dst, 
             return planes[:, t, s0:s1]
 
         upper_words = grouped[:].bitcast(F32).rearrange("p (n u) -> p u n", u=2)[:, 1, :]
-        parked = {EG * g + 2: upper_words[:, LAST + g * LIST_STEP : LAST + g * LIST_STEP + 1] for g in (0, 1)}
+        e_first, e_second = FIRST // N + 2, SECOND // N + 2
+        parked = {
+            e_first: pairs[:].bitcast(F32)[:, 2 * G + FIRST : 2 * G + FIRST + 1],
+            e_second: upper_words[:, LAST : LAST + 1],
+        }
 
         def round_plane(t):
             c0 = 0
@@ -162,31 +172,28 @@ def tile_moe_two_lin_gelu_kernel(tc, xT, w_words, w_scales, b, gate, offs, dst, 
             s1 = s0 + G
             nc.vector.tensor_tensor(out_t[:].indirect(dst_t[:, s0 // 16 : s1 // 16]), y[:, s0:s1], gate_t[:, s0:s1], mult)
 
-        for t in (0, 1):
+        for t in range(3):
             round_plane(t)
-            gather_vector(t, FIRST, THIRD)
-            gather_vector(t, THIRD, LAST)
-            gather_scalar(t, LAST, SLOTS)
-        round_plane(2)
-        gather_vector(2, FIRST, THIRD)
-        gather_vector(2, THIRD, LAST)
+            gather_vector(t, THIRD, FIRST + G)
+            gather_vector(t, SECOND, SECOND + G)
+            if t < 2:
+                gather_scalar(t, LAST, SLOTS)
         round_plane(3)
         gather_vector(3, FIRST, FIRST + G)
         gather_scalar(3, SECOND, SECOND + G)
-        for e in sorted(parked):
-            nc.gpsimd.tensor_copy(out=parked[e], in_=b_t[:, e : e + 1])
+        nc.gpsimd.tensor_copy(out=parked[e_second], in_=b_t[:, e_second : e_second + 1])
 
-        for e in range(EG + WEAVE_AHEAD):
-            if e >= WEAVE_AHEAD:
-                quantize_and_multiply((e - WEAVE_AHEAD) * N, (e - WEAVE_AHEAD + 1) * N)
-            if e < EG:
-                weave(nc.vector.tensor_copy, I32, e * N, (e + 1) * N)
-        weave(nc.scalar.copy, U32, SECOND, SECOND + G // 2)
-        weave(nc.vector.tensor_copy, I32, SECOND + G // 2, SECOND + G)
-        quantize_and_multiply(SECOND, SECOND + G // 2)
-        quantize_and_multiply(SECOND + G // 2, SECOND + G)
+        for i in range(EG + WEAVE_AHEAD):
+            if i >= WEAVE_AHEAD:
+                s0 = FIRST + (i - WEAVE_AHEAD) * N
+                quantize_and_multiply(s0, s0 + N)
+            if i < EG:
+                weave(nc.vector.tensor_copy, I32, FIRST + i * N, FIRST + (i + 1) * N)
+        nc.vector.tensor_copy(out=parked[e_first], in_=b_t[:, e_first : e_first + 1])
+        quantize_and_multiply(SECOND, SECOND + G)
         activate(FIRST)
         gather_scalar(3, THIRD, THIRD + G + LIST_STEP)
+        weave(nc.scalar.copy, U32, THIRD, THIRD + G)
         activate(SECOND)
 
         scatter(FIRST)

@@ -42,7 +42,7 @@ def tile_moe_two_lin_gelu_kernel(tc, xT, w_words, w_scales, b, gate, offs, dst, 
         raw = [keep.tile([P, T], F32, name=f"raw{t}") for t in range(4)]
         half = [keep.tile([P, T], BF16, name=f"half{t}") for t in range(4)]
         grouped = keep.tile([P, 4 * SLOTS], BF16, name="grouped", align_bytes=64)
-        pairs = keep.tile([P, 4 * 2 * G], BF16, name="pairs", align_bytes=64)
+        pairs = keep.tile([P, 4 * LAST], BF16, name="pairs", align_bytes=64)
         codes = keep.tile([P, SLOTS], U32, name="codes", align_bytes=64)
         scales = keep.tile([P, SLOTS], U8, name="scales", align_bytes=64)
         w_t = keep.tile([P, E, 2 * N], U8, name="w_t", align_bytes=64)
@@ -109,14 +109,14 @@ def tile_moe_two_lin_gelu_kernel(tc, xT, w_words, w_scales, b, gate, offs, dst, 
         pair_planes = pairs[:].rearrange("p (u n v) -> p u v n", u=2, v=2)
 
         def place(t, s0, s1):
-            if s1 <= 2 * G:
+            if s1 <= LAST:
                 return pair_planes[:, t // 2, t % 2, s0:s1]
             return planes[:, t, s0:s1]
 
         upper_words = grouped[:].bitcast(F32).rearrange("p (n u) -> p u n", u=2)[:, 1, :]
         e_first, e_second = FIRST // N + 2, SECOND // N + 2
         parked = {
-            e_first: pairs[:].bitcast(F32)[:, 2 * G + FIRST : 2 * G + FIRST + 1],
+            e_first: pairs[:].bitcast(F32)[:, LAST + FIRST : LAST + FIRST + 1],
             e_second: upper_words[:, LAST : LAST + 1],
         }
 
@@ -174,8 +174,7 @@ def tile_moe_two_lin_gelu_kernel(tc, xT, w_words, w_scales, b, gate, offs, dst, 
 
         for t in range(3):
             round_plane(t)
-            gather_vector(t, THIRD, FIRST + G)
-            gather_vector(t, SECOND, SECOND + G)
+            gather_vector(t, 0, LAST)
             if t < 2:
                 gather_scalar(t, LAST, SLOTS)
         round_plane(3)
@@ -190,7 +189,10 @@ def tile_moe_two_lin_gelu_kernel(tc, xT, w_words, w_scales, b, gate, offs, dst, 
             if i < EG:
                 weave(nc.vector.tensor_copy, I32, FIRST + i * N, FIRST + (i + 1) * N)
         nc.vector.tensor_copy(out=parked[e_first], in_=b_t[:, e_first : e_first + 1])
-        quantize_and_multiply(SECOND, SECOND + G)
+        weave(nc.scalar.copy, U32, SECOND, SECOND + G // 2)
+        weave(nc.vector.tensor_copy, I32, SECOND + G // 2, SECOND + G)
+        quantize_and_multiply(SECOND, SECOND + G // 2)
+        quantize_and_multiply(SECOND + G // 2, SECOND + G)
         activate(FIRST)
         gather_scalar(3, THIRD, THIRD + G + LIST_STEP)
         weave(nc.scalar.copy, U32, THIRD, THIRD + G)

@@ -16,7 +16,7 @@ P = 128
 G = 512
 EG = G // N
 
-FIRST, SECOND, THIRD, LAST = G, 2 * G, 0, 3 * G
+FIRST, SECOND, THIRD, LAST = 0, G, 2 * G, 3 * G
 
 LOADS = (
     ((("gpsimd", 1920), ("scalar", T)),),
@@ -25,8 +25,8 @@ LOADS = (
     ((("gpsimd", 1088), ("scalar", 2304)), (("vector", 3072), ("scalar", 3584)), (("scalar", 3872), ("gpsimd", T))),
 )
 
-LIST_STEP = 32
 WEAVE_AHEAD = 3
+LENT = THIRD + N // 2
 
 
 def tile_moe_two_lin_gelu_kernel(tc, xT, w_words, w_scales, b, gate, offs, dst, out):
@@ -51,16 +51,11 @@ def tile_moe_two_lin_gelu_kernel(tc, xT, w_words, w_scales, b, gate, offs, dst, 
         gate_t = keep.tile([P, SLOTS], F32, name="gate_t")
         y = keep.tile([P, SLOTS], F32, name="y")
         out_t = keep.tile([P, T], F32, name="out_t")
+        saved = keep.tile([P, 1], BF16, name="saved")
         warm = keep.tile([P, 1], F32, name="warm")
-        acc = {}
-        for s0 in (FIRST, SECOND, THIRD, LAST):
-            if s0 == FIRST:
-                parts = [psum.tile([P, N], F32, name=f"first{i}")[:] for i in range(EG)]
-            else:
-                bank = psum.tile([P, G], F32, name=f"bank{s0}")
-                parts = [bank[:, i * N : (i + 1) * N] for i in range(EG)]
-            for i in range(EG):
-                acc[s0 // N + i] = parts[i]
+        first = [psum.tile([P, N], F32, name=f"first{e}") for e in range(EG)]
+        later = [psum.tile([P, G], F32, name=f"later{g}") for g in range(3)]
+        acc = [tile[:] for tile in first] + [tile[:, i * N : (i + 1) * N] for tile in later for i in range(EG)]
 
         x_rows = xT.rearrange("(p t) w -> p t w", t=4)
         ws_rows = w_scales.bitcast(I32).rearrange("e a q n -> (a q) e n")
@@ -96,11 +91,11 @@ def tile_moe_two_lin_gelu_kernel(tc, xT, w_words, w_scales, b, gate, offs, dst, 
         load_weights(FIRST + 2 * N, FIRST + G)
         nc.sync.dma_start(dst_t[:], dst)
         load_gate(FIRST, FIRST + G)
-        load_scales(SECOND, SLOTS)
+        load_scales(SECOND, SECOND + G)
         load_weights(SECOND, SECOND + 2 * N)
         load_weights(SECOND + 2 * N, SECOND + G)
         load_gate(SECOND, SECOND + G)
-        load_scales(THIRD, THIRD + G)
+        load_scales(THIRD, SLOTS)
         for s0 in (THIRD, LAST):
             load_weights(s0, s0 + G)
             load_gate(s0, s0 + G)
@@ -114,10 +109,9 @@ def tile_moe_two_lin_gelu_kernel(tc, xT, w_words, w_scales, b, gate, offs, dst, 
             return planes[:, t, s0:s1]
 
         upper_words = grouped[:].bitcast(F32).rearrange("p (n u) -> p u n", u=2)[:, 1, :]
-        e_first, e_second = FIRST // N + 2, SECOND // N + 2
         parked = {
-            e_first: pairs[:].bitcast(F32)[:, LAST + FIRST : LAST + FIRST + 1],
-            e_second: upper_words[:, LAST : LAST + 1],
+            FIRST // N + 2: pairs[:].bitcast(F32)[:, LAST + LENT : LAST + LENT + 1],
+            SECOND // N + 2: upper_words[:, LAST : LAST + 1],
         }
 
         def round_plane(t):
@@ -177,9 +171,11 @@ def tile_moe_two_lin_gelu_kernel(tc, xT, w_words, w_scales, b, gate, offs, dst, 
             gather_vector(t, 0, LAST)
             if t < 2:
                 gather_scalar(t, LAST, SLOTS)
+        nc.vector.tensor_copy(out=saved[:], in_=place(2, LENT, LENT + 1))
         round_plane(3)
         gather_vector(3, FIRST, FIRST + G)
         gather_scalar(3, SECOND, SECOND + G)
+        e_first, e_second = sorted(parked)
         nc.gpsimd.tensor_copy(out=parked[e_second], in_=b_t[:, e_second : e_second + 1])
 
         for i in range(EG + WEAVE_AHEAD):
@@ -194,8 +190,9 @@ def tile_moe_two_lin_gelu_kernel(tc, xT, w_words, w_scales, b, gate, offs, dst, 
         quantize_and_multiply(SECOND, SECOND + G // 2)
         quantize_and_multiply(SECOND + G // 2, SECOND + G)
         activate(FIRST)
-        gather_scalar(3, THIRD, THIRD + G + LIST_STEP)
-        weave(nc.scalar.copy, U32, THIRD, THIRD + G)
+        gather_scalar(3, THIRD, LAST)
+        nc.scalar.copy(out=place(2, LENT, LENT + 1), in_=saved[:])
+        weave(nc.scalar.copy, U32, THIRD, LAST)
         activate(SECOND)
 
         scatter(FIRST)

@@ -86,19 +86,14 @@ def tile_moe_two_lin_gelu_kernel(tc, xT, w_words, w_scales, b, gate, offs, dst, 
             nc.sync.dma_start(out=gate_t[:, s0:s1], in_=gate[:, s0:s1])
 
         nc.sync.dma_start(b_t[:], b)
-        load_scales(FIRST, FIRST + G)
-        load_weights(FIRST, FIRST + 2 * N)
-        load_weights(FIRST + 2 * N, FIRST + G)
+        load_scales(FIRST, SECOND)
+        load_weights(FIRST, SECOND)
         nc.sync.dma_start(dst_t[:], dst)
-        load_gate(FIRST, FIRST + G)
-        load_scales(SECOND, SECOND + G)
-        load_weights(SECOND, SECOND + 2 * N)
-        load_weights(SECOND + 2 * N, SECOND + G)
-        load_gate(SECOND, SECOND + G)
-        load_scales(THIRD, SLOTS)
-        for s0 in (THIRD, LAST):
-            load_weights(s0, s0 + G)
-            load_gate(s0, s0 + G)
+        load_gate(FIRST, SECOND)
+        load_scales(SECOND, SLOTS)
+        for s0, s1 in ((SECOND, THIRD), (THIRD, SLOTS)):
+            load_weights(s0, s1)
+            load_gate(s0, s1)
 
         planes = grouped[:].rearrange("p (n t) -> p t n", t=4)
         pair_planes = pairs[:].rearrange("p (u n v) -> p u v n", u=2, v=2)

@@ -22,7 +22,7 @@ LOADS = (
     ((("gpsimd", 1920), ("scalar", T)),),
     ((("gpsimd", 1920), ("scalar", T)),),
     ((("gpsimd", 1920), ("scalar", T)),),
-    ((("gpsimd", 1088), ("scalar", 2304)), (("vector", 3072), ("scalar", 3584)), (("scalar", 3872), ("gpsimd", T))),
+    ((("gpsimd", 896), ("scalar", 2176)), (("vector", 3072), ("scalar", 3584)), (("scalar", 3904), ("gpsimd", T))),
 )
 
 WEAVE_AHEAD = 3

@@ -15,18 +15,11 @@ FP4X4 = mybir.dt.float4_e2m1fn_x4
 P = 128
 G = 512
 EG = G // N
+GROUPS = SLOTS // G
 
-FIRST, SECOND, THIRD, LAST = 0, G, 2 * G, 3 * G
-
-LOADS = (
-    ((("gpsimd", 1920), ("scalar", T)),),
-    ((("gpsimd", 1920), ("scalar", T)),),
-    ((("gpsimd", 1920), ("scalar", T)),),
-    ((("gpsimd", 896), ("scalar", 2176)), (("vector", 3072), ("scalar", 3584)), (("scalar", 3904), ("gpsimd", T))),
-)
-
-WEAVE_AHEAD = 3
-LENT = THIRD + N // 2
+DIRECT = 1280
+SCALAR_PLACES = 192
+HELD = 3
 
 
 def tile_moe_two_lin_gelu_kernel(tc, xT, w_words, w_scales, b, gate, offs, dst, out):
@@ -34,24 +27,21 @@ def tile_moe_two_lin_gelu_kernel(tc, xT, w_words, w_scales, b, gate, offs, dst, 
     gelu = mybir.ActivationFunctionType.Gelu_apprx_tanh
     copy = mybir.ActivationFunctionType.Copy
     mult = mybir.AluOpType.mult
-    add = mybir.AluOpType.add
 
     with tc.tile_pool(name="keep", bufs=1) as keep, tc.psum_pool(name="psum", bufs=1) as psum:
         offs_t = keep.tile([P, SLOTS // 16], U16, name="offs_t")
         dst_t = keep.tile([P, SLOTS // 16], U16, name="dst_t")
         raw = [keep.tile([P, T], F32, name=f"raw{t}") for t in range(4)]
-        half = [keep.tile([P, T], BF16, name=f"half{t}") for t in range(4)]
         grouped = keep.tile([P, 4 * SLOTS], BF16, name="grouped", align_bytes=64)
-        pairs = keep.tile([P, 4 * LAST], BF16, name="pairs", align_bytes=64)
+        early = keep.tile([P, 2 * (SLOTS - DIRECT)], BF16, name="early")
+        late = [keep.tile([P, 2 * G + 2 * E], BF16, name=f"late{g}") for g in range(GROUPS)]
         codes = keep.tile([P, SLOTS], U32, name="codes", align_bytes=64)
         scales = keep.tile([P, SLOTS], U8, name="scales", align_bytes=64)
         w_t = keep.tile([P, E, 2 * N], U8, name="w_t", align_bytes=64)
         ws_t = keep.tile([P, E, N], U8, name="ws_t", align_bytes=64)
-        b_t = keep.tile([P, E], F32, name="b_t")
         gate_t = keep.tile([P, SLOTS], F32, name="gate_t")
         y = keep.tile([P, SLOTS], F32, name="y")
         out_t = keep.tile([P, T], F32, name="out_t")
-        saved = keep.tile([P, 1], BF16, name="saved")
         warm = keep.tile([P, 1], F32, name="warm")
         first = [psum.tile([P, N], F32, name=f"first{e}") for e in range(EG)]
         later = [psum.tile([P, G], F32, name=f"later{g}") for g in range(3)]
@@ -61,19 +51,18 @@ def tile_moe_two_lin_gelu_kernel(tc, xT, w_words, w_scales, b, gate, offs, dst, 
         ws_rows = w_scales.bitcast(I32).rearrange("e a q n -> (a q) e n")
         w_rows = w_words.bitcast(I32).rearrange("e a p n -> p (e a) n")
 
+        bias_first = late[2][:].bitcast(F32)[:, G - HELD : G - HELD + EG]
+        bias_rest = late[3][:].bitcast(F32)[:, G - HELD : G - HELD + E - EG]
+
         nc.vector.memset(warm[:], 0.0)
         nc.scalar.activation(out=warm[:], in_=warm[:], func=gelu)
         nc.vector.memset(ws_t[:].rearrange("p e n -> p (e n)").bitcast(I32), 0)
         nc.vector.memset(out_t[:], 0.0)
 
         for t in range(4):
-            c0 = 0
-            for shares in LOADS[t]:
-                c1 = shares[-1][1]
-                nc.sync.dma_start(out=raw[t][:, c0:c1], in_=x_rows[:, t, c0:c1])
-                if t == 0 and c0 == 0:
-                    nc.sync.dma_start(offs_t[:], offs)
-                c0 = c1
+            nc.sync.dma_start(out=raw[t][:], in_=x_rows[:, t, :])
+            if t == 0:
+                nc.sync.dma_start(offs_t[:], offs)
 
         def load_scales(s0, s1):
             for r in range(4):
@@ -85,58 +74,38 @@ def tile_moe_two_lin_gelu_kernel(tc, xT, w_words, w_scales, b, gate, offs, dst, 
         def load_gate(s0, s1):
             nc.sync.dma_start(out=gate_t[:, s0:s1], in_=gate[:, s0:s1])
 
-        nc.sync.dma_start(b_t[:], b)
-        load_scales(FIRST, SECOND)
-        load_weights(FIRST, SECOND)
+        load_scales(0, G)
+        load_weights(0, G)
+        nc.sync.dma_start(bias_first, b[:, :EG])
+        load_gate(0, G)
         nc.sync.dma_start(dst_t[:], dst)
-        load_gate(FIRST, SECOND)
-        load_scales(SECOND, SLOTS)
-        for s0, s1 in ((SECOND, THIRD), (THIRD, SLOTS)):
+        load_scales(G, SLOTS)
+        nc.sync.dma_start(bias_rest, b[:, EG:])
+        for s0, s1 in ((G, 2 * G), (2 * G, SLOTS)):
             load_weights(s0, s1)
             load_gate(s0, s1)
 
-        planes = grouped[:].rearrange("p (n t) -> p t n", t=4)
-        pair_planes = pairs[:].rearrange("p (u n v) -> p u v n", u=2, v=2)
+        words = grouped[:].rearrange("p (n t) -> p n t", t=4)
 
-        def place(t, s0, s1):
-            if s1 <= LAST:
-                return pair_planes[:, t // 2, t % 2, s0:s1]
-            return planes[:, t, s0:s1]
+        def listed(t, s0, s1):
+            return raw[t][:].indirect(offs_t[:, s0 // 16 : s1 // 16])
 
-        upper_words = grouped[:].bitcast(F32).rearrange("p (n u) -> p u n", u=2)[:, 1, :]
-        parked = {
-            FIRST // N + 2: pairs[:].bitcast(F32)[:, LAST + LENT : LAST + LENT + 1],
-            SECOND // N + 2: upper_words[:, LAST : LAST + 1],
-        }
-
-        def round_plane(t):
-            c0 = 0
-            for shares in LOADS[t]:
-                for engine, c1 in shares:
-                    if engine == "scalar":
-                        nc.scalar.copy(out=half[t][:, c0:c1], in_=raw[t][:, c0:c1])
-                    elif engine == "gpsimd":
-                        nc.gpsimd.tensor_scalar(out=half[t][:, c0:c1], in0=raw[t][:, c0:c1], scalar1=1.0, scalar2=0.0, op0=mult, op1=add)
-                    else:
-                        nc.vector.tensor_copy(out=half[t][:, c0:c1], in_=raw[t][:, c0:c1])
-                    c0 = c1
+        def late_plane(t, s0, s1):
+            c0 = (t - 2) * G + s0 % G
+            return late[s0 // G][:, c0 : c0 + s1 - s0]
 
         def gather_vector(t, s0, s1):
-            nc.vector.tensor_copy(place(t, s0, s1), raw[t][:].indirect(offs_t[:, s0 // 16 : s1 // 16]))
+            nc.vector.tensor_copy(late_plane(t, s0, s1), listed(t, s0, s1))
 
         def gather_scalar(t, s0, s1):
-            nc.scalar.activation(place(t, s0, s1), half[t][:].indirect(offs_t[:, s0 // 16 : s1 // 16]), copy)
+            nc.scalar.activation(late_plane(t, s0, s1), listed(t, s0, s1), copy)
 
-        def weave(move, dtype, s0, s1):
-            move(
-                out=grouped[:].bitcast(dtype).rearrange("p (n u) -> p n u", u=2)[:, s0:s1, :],
-                in_=pairs[:].bitcast(dtype).rearrange("p (u n) -> p n u", u=2)[:, s0:s1, :],
-            )
+        def place(move, s0, s1):
+            pairs = late[s0 // G][:, : 2 * G].rearrange("p (u n) -> p n u", u=2)
+            move(out=words[:, s0:s1, 2:4], in_=pairs[:, s0 % G : s0 % G + s1 - s0, :])
 
-        def quantize(s0, s1):
+        def quantize_and_multiply(s0, s1):
             nc.vector.quantize_mx(out=codes[:, s0:s1].bitcast(FP8X4), scales=scales[:, s0:s1], in_=grouped[:, 4 * s0 : 4 * s1])
-
-        def multiply(s0, s1):
             for e in range(s0 // N, s1 // N):
                 nc.tensor.matmul_mx(
                     out=acc[e],
@@ -148,56 +117,49 @@ def tile_moe_two_lin_gelu_kernel(tc, xT, w_words, w_scales, b, gate, offs, dst, 
                     stop=True,
                 )
 
-        def quantize_and_multiply(s0, s1):
-            quantize(s0, s1)
-            multiply(s0, s1)
-
-        def activate(s0):
-            for e in range(s0 // N, s0 // N + EG):
-                bias = parked.get(e, b_t[:, e : e + 1])
+        def activate(g):
+            for e in range(g * EG, (g + 1) * EG):
+                bias = bias_first[:, e : e + 1] if e < EG else bias_rest[:, e - EG : e - EG + 1]
                 nc.scalar.activation(out=y[:, e * N : (e + 1) * N], in_=acc[e], func=gelu, bias=bias)
 
-        def scatter(s0):
-            s1 = s0 + G
+        def scatter(g):
+            s0, s1 = g * G, (g + 1) * G
             nc.vector.tensor_tensor(out_t[:].indirect(dst_t[:, s0 // 16 : s1 // 16]), y[:, s0:s1], gate_t[:, s0:s1], mult)
 
-        for t in range(3):
-            round_plane(t)
-            gather_vector(t, 0, LAST)
-            if t < 2:
-                gather_scalar(t, LAST, SLOTS)
-        nc.vector.tensor_copy(out=saved[:], in_=place(2, LENT, LENT + 1))
-        round_plane(3)
-        gather_vector(3, FIRST, FIRST + G)
-        gather_scalar(3, SECOND, SECOND + G)
-        e_first, e_second = sorted(parked)
-        nc.gpsimd.tensor_copy(out=parked[e_second], in_=b_t[:, e_second : e_second + 1])
+        rest = SLOTS - DIRECT
+        for t in range(2):
+            nc.vector.tensor_copy(words[:, :DIRECT, t], listed(t, 0, DIRECT))
+            nc.scalar.activation(early[:, t * rest : (t + 1) * rest], listed(t, DIRECT, SLOTS), copy)
+        nc.scalar.copy(out=words[:, DIRECT:, 0:2], in_=early[:].rearrange("p (u n) -> p n u", u=2))
+        for g in range(2):
+            gather_vector(2, g * G, (g + 1) * G)
+            gather_scalar(2, (g + 2) * G, (g + 3) * G)
 
-        for i in range(EG + WEAVE_AHEAD):
-            if i >= WEAVE_AHEAD:
-                s0 = FIRST + (i - WEAVE_AHEAD) * N
-                quantize_and_multiply(s0, s0 + N)
-            if i < EG:
-                weave(nc.vector.tensor_copy, I32, FIRST + i * N, FIRST + (i + 1) * N)
-        nc.vector.tensor_copy(out=parked[e_first], in_=b_t[:, e_first : e_first + 1])
-        weave(nc.scalar.copy, U32, SECOND, SECOND + G // 2)
-        weave(nc.vector.tensor_copy, I32, SECOND + G // 2, SECOND + G)
-        quantize_and_multiply(SECOND, SECOND + G // 2)
-        quantize_and_multiply(SECOND + G // 2, SECOND + G)
-        activate(FIRST)
-        gather_scalar(3, THIRD, LAST)
-        nc.scalar.copy(out=place(2, LENT, LENT + 1), in_=saved[:])
-        weave(nc.scalar.copy, U32, THIRD, LAST)
-        activate(SECOND)
+        gather_vector(3, 0, N)
+        gather_vector(3, N, 2 * N)
+        gather_scalar(3, 2 * N, G)
+        gather_scalar(3, G, G + G // 2)
+        gather_scalar(3, G + G // 2, 2 * G)
+        place(nc.vector.tensor_copy, 0, N)
+        place(nc.vector.tensor_copy, N, 2 * N)
+        quantize_and_multiply(0, N)
+        place(nc.vector.tensor_copy, 2 * N, 3 * N)
+        place(nc.vector.tensor_copy, 3 * N, G)
+        for e in range(1, EG):
+            quantize_and_multiply(e * N, (e + 1) * N)
+        place(nc.scalar.copy, G, G + SCALAR_PLACES)
+        place(nc.vector.tensor_copy, G + SCALAR_PLACES, 2 * G)
+        quantize_and_multiply(G, G + N)
+        quantize_and_multiply(G + N, 2 * G)
+        activate(0)
 
-        scatter(FIRST)
-        quantize_and_multiply(THIRD, THIRD + G)
-        gather_scalar(2, LAST, LAST + G)
-        gather_scalar(3, LAST, LAST + G)
-        activate(THIRD)
-        scatter(SECOND)
-        quantize_and_multiply(LAST, LAST + G)
-        activate(LAST)
-        scatter(THIRD)
-        scatter(LAST)
+        for g in range(GROUPS):
+            if g + 2 < GROUPS:
+                gather_scalar(3, (g + 2) * G, (g + 3) * G)
+                place(nc.scalar.copy, (g + 2) * G, (g + 3) * G)
+            if g + 1 < GROUPS:
+                activate(g + 1)
+            scatter(g)
+            if g + 2 < GROUPS:
+                quantize_and_multiply((g + 2) * G, (g + 3) * G)
         nc.sync.dma_start(out, out_t[:])

@@ -19,7 +19,6 @@ GROUPS = SLOTS // G
 
 DIRECT = 1280
 SCALAR_PLACES = 192
-HELD = 3
 
 
 def tile_moe_two_lin_gelu_kernel(tc, xT, w_words, w_scales, b, gate, offs, dst, out):
@@ -34,11 +33,12 @@ def tile_moe_two_lin_gelu_kernel(tc, xT, w_words, w_scales, b, gate, offs, dst, 
         raw = [keep.tile([P, T], F32, name=f"raw{t}") for t in range(4)]
         grouped = keep.tile([P, 4 * SLOTS], BF16, name="grouped", align_bytes=64)
         early = keep.tile([P, 2 * (SLOTS - DIRECT)], BF16, name="early")
-        late = [keep.tile([P, 2 * G + 2 * E], BF16, name=f"late{g}") for g in range(GROUPS)]
+        late = [keep.tile([P, 2 * G], BF16, name=f"late{g}") for g in range(GROUPS)]
         codes = keep.tile([P, SLOTS], U32, name="codes", align_bytes=64)
         scales = keep.tile([P, SLOTS], U8, name="scales", align_bytes=64)
         w_t = keep.tile([P, E, 2 * N], U8, name="w_t", align_bytes=64)
         ws_t = keep.tile([P, E, N], U8, name="ws_t", align_bytes=64)
+        b_t = keep.tile([P, E - 2 * EG], F32, name="b_t")
         gate_t = keep.tile([P, SLOTS], F32, name="gate_t")
         y = keep.tile([P, SLOTS], F32, name="y")
         out_t = keep.tile([P, T], F32, name="out_t")
@@ -51,8 +51,9 @@ def tile_moe_two_lin_gelu_kernel(tc, xT, w_words, w_scales, b, gate, offs, dst, 
         ws_rows = w_scales.bitcast(I32).rearrange("e a q n -> (a q) e n")
         w_rows = w_words.bitcast(I32).rearrange("e a p n -> p (e a) n")
 
-        bias_first = late[2][:].bitcast(F32)[:, G - HELD : G - HELD + EG]
-        bias_rest = late[3][:].bitcast(F32)[:, G - HELD : G - HELD + E - EG]
+        middle = 3 * G // 4
+        bias = [late[g + 2][:].bitcast(F32)[:, middle - EG // 2 : middle + EG // 2] for g in range(2)]
+        bias = bias + [b_t[:, :EG], b_t[:, EG:]]
 
         nc.vector.memset(warm[:], 0.0)
         nc.scalar.activation(out=warm[:], in_=warm[:], func=gelu)
@@ -76,14 +77,15 @@ def tile_moe_two_lin_gelu_kernel(tc, xT, w_words, w_scales, b, gate, offs, dst, 
 
         load_scales(0, G)
         load_weights(0, G)
-        nc.sync.dma_start(bias_first, b[:, :EG])
+        nc.sync.dma_start(bias[0], b[:, :EG])
         load_gate(0, G)
         nc.sync.dma_start(dst_t[:], dst)
         load_scales(G, SLOTS)
-        nc.sync.dma_start(bias_rest, b[:, EG:])
+        nc.sync.dma_start(bias[1], b[:, EG : 2 * EG])
         for s0, s1 in ((G, 2 * G), (2 * G, SLOTS)):
             load_weights(s0, s1)
             load_gate(s0, s1)
+        nc.sync.dma_start(b_t[:], b[:, 2 * EG :])
 
         words = grouped[:].rearrange("p (n t) -> p n t", t=4)
 
@@ -118,9 +120,9 @@ def tile_moe_two_lin_gelu_kernel(tc, xT, w_words, w_scales, b, gate, offs, dst, 
                 )
 
         def activate(g):
-            for e in range(g * EG, (g + 1) * EG):
-                bias = bias_first[:, e : e + 1] if e < EG else bias_rest[:, e - EG : e - EG + 1]
-                nc.scalar.activation(out=y[:, e * N : (e + 1) * N], in_=acc[e], func=gelu, bias=bias)
+            for i in range(EG):
+                e = g * EG + i
+                nc.scalar.activation(out=y[:, e * N : (e + 1) * N], in_=acc[e], func=gelu, bias=bias[g][:, i : i + 1])
 
         def scatter(g):
             s0, s1 = g * G, (g + 1) * G
@@ -142,24 +144,25 @@ def tile_moe_two_lin_gelu_kernel(tc, xT, w_words, w_scales, b, gate, offs, dst, 
         gather_scalar(3, G + G // 2, 2 * G)
         place(nc.vector.tensor_copy, 0, N)
         place(nc.vector.tensor_copy, N, 2 * N)
-        quantize_and_multiply(0, N)
-        place(nc.vector.tensor_copy, 2 * N, 3 * N)
-        place(nc.vector.tensor_copy, 3 * N, G)
-        for e in range(1, EG):
-            quantize_and_multiply(e * N, (e + 1) * N)
+        place(nc.vector.tensor_copy, 2 * N, G)
+        quantize_and_multiply(0, 2 * N)
+        quantize_and_multiply(2 * N, G)
+        place(nc.vector.tensor_copy, G + SCALAR_PLACES, G + G // 2)
         place(nc.scalar.copy, G, G + SCALAR_PLACES)
-        place(nc.vector.tensor_copy, G + SCALAR_PLACES, 2 * G)
-        quantize_and_multiply(G, G + N)
-        quantize_and_multiply(G + N, 2 * G)
+        place(nc.vector.tensor_copy, G + G // 2, 2 * G)
+        quantize_and_multiply(G, G + G // 2)
+        quantize_and_multiply(G + G // 2, 2 * G)
         activate(0)
 
         for g in range(GROUPS):
-            if g + 2 < GROUPS:
-                gather_scalar(3, (g + 2) * G, (g + 3) * G)
-                place(nc.scalar.copy, (g + 2) * G, (g + 3) * G)
+            halves = range((g + 2) * G, min(g + 3, GROUPS) * G, G // 2)
+            for s0 in halves:
+                gather_scalar(3, s0, s0 + G // 2)
+            for s0 in halves:
+                place(nc.scalar.copy, s0, s0 + G // 2)
             if g + 1 < GROUPS:
                 activate(g + 1)
             scatter(g)
-            if g + 2 < GROUPS:
-                quantize_and_multiply((g + 2) * G, (g + 3) * G)
+            for s0 in halves:
+                quantize_and_multiply(s0, s0 + G // 2)
         nc.sync.dma_start(out, out_t[:])

@@ -18,7 +18,7 @@ EG = G // N
 GROUPS = SLOTS // G
 
 DIRECT = 1280
-SCALAR_PLACES = 192
+SCALAR_FIRST = 64
 
 
 def tile_moe_two_lin_gelu_kernel(tc, xT, w_words, w_scales, b, gate, offs, dst, out):
@@ -141,14 +141,15 @@ def tile_moe_two_lin_gelu_kernel(tc, xT, w_words, w_scales, b, gate, offs, dst, 
         gather_vector(3, N, 2 * N)
         gather_scalar(3, 2 * N, G)
         gather_scalar(3, G, G + G // 2)
+        place(nc.scalar.copy, G - SCALAR_FIRST, G)
         gather_scalar(3, G + G // 2, 2 * G)
+        place(nc.scalar.copy, G, G + N)
         place(nc.vector.tensor_copy, 0, N)
         place(nc.vector.tensor_copy, N, 2 * N)
-        place(nc.vector.tensor_copy, 2 * N, G)
-        quantize_and_multiply(0, 2 * N)
-        quantize_and_multiply(2 * N, G)
-        place(nc.vector.tensor_copy, G + SCALAR_PLACES, G + G // 2)
-        place(nc.scalar.copy, G, G + SCALAR_PLACES)
+        place(nc.vector.tensor_copy, 2 * N, G - SCALAR_FIRST)
+        for e in range(EG):
+            quantize_and_multiply(e * N, (e + 1) * N)
+        place(nc.vector.tensor_copy, G + N, G + G // 2)
         place(nc.vector.tensor_copy, G + G // 2, 2 * G)
         quantize_and_multiply(G, G + G // 2)
         quantize_and_multiply(G + G // 2, 2 * G)

@@ -19,6 +19,7 @@ GROUPS = SLOTS // G
 
 DIRECT = 1280
 SCALAR_FIRST = 64
+SCALAR_SECOND = 96
 
 
 def tile_moe_two_lin_gelu_kernel(tc, xT, w_words, w_scales, b, gate, offs, dst, out):
@@ -142,15 +143,17 @@ def tile_moe_two_lin_gelu_kernel(tc, xT, w_words, w_scales, b, gate, offs, dst, 
         gather_scalar(3, 2 * N, G)
         gather_scalar(3, G, G + G // 2)
         place(nc.scalar.copy, G - SCALAR_FIRST, G)
-        gather_scalar(3, G + G // 2, 2 * G)
-        place(nc.scalar.copy, G, G + N)
+        gather_scalar(3, 2 * G - 2 * N, 2 * G - N)
+        gather_scalar(3, 2 * G - N, 2 * G)
+        place(nc.scalar.copy, G, G + SCALAR_SECOND)
         place(nc.vector.tensor_copy, 0, N)
         place(nc.vector.tensor_copy, N, 2 * N)
         place(nc.vector.tensor_copy, 2 * N, G - SCALAR_FIRST)
         for e in range(EG):
             quantize_and_multiply(e * N, (e + 1) * N)
-        place(nc.vector.tensor_copy, G + N, G + G // 2)
-        place(nc.vector.tensor_copy, G + G // 2, 2 * G)
+        place(nc.vector.tensor_copy, G + SCALAR_SECOND, G + G // 2)
+        place(nc.vector.tensor_copy, 2 * G - 2 * N, 2 * G - N)
+        place(nc.vector.tensor_copy, 2 * G - N, 2 * G)
         quantize_and_multiply(G, G + G // 2)
         quantize_and_multiply(G + G // 2, 2 * G)
         activate(0)

@@ -61,11 +61,6 @@ def tile_moe_two_lin_gelu_kernel(tc, xT, w_words, w_scales, b, gate, offs, dst, 
         nc.vector.memset(ws_t[:].rearrange("p e n -> p (e n)").bitcast(I32), 0)
         nc.vector.memset(out_t[:], 0.0)
 
-        for t in range(4):
-            nc.sync.dma_start(out=raw[t][:], in_=x_rows[:, t, :])
-            if t == 0:
-                nc.sync.dma_start(offs_t[:], offs)
-
         def load_scales(s0, s1):
             for r in range(4):
                 nc.sync.dma_start(out=ws_t[r:P:32, s0 // N : s1 // N, :].bitcast(I32), in_=ws_rows[r:16:4, s0 // N : s1 // N])
@@ -76,7 +71,11 @@ def tile_moe_two_lin_gelu_kernel(tc, xT, w_words, w_scales, b, gate, offs, dst, 
         def load_gate(s0, s1):
             nc.sync.dma_start(out=gate_t[:, s0:s1], in_=gate[:, s0:s1])
 
-        load_scales(0, G)
+        for t in range(4):
+            nc.sync.dma_start(out=raw[t][:], in_=x_rows[:, t, :])
+            if t == 0:
+                nc.sync.dma_start(offs_t[:], offs)
+                load_scales(0, G)
         load_weights(0, G)
         nc.sync.dma_start(bias[0], b[:, :EG])
         load_gate(0, G)

@@ -18,6 +18,7 @@ EG = G // N
 GROUPS = SLOTS // G
 
 DIRECT = 1280
+EARLY_ROWS = 2
 SCALAR_FIRST = 64
 SCALAR_SECOND = 96
 
@@ -61,8 +62,8 @@ def tile_moe_two_lin_gelu_kernel(tc, xT, w_words, w_scales, b, gate, offs, dst, 
         nc.vector.memset(ws_t[:].rearrange("p e n -> p (e n)").bitcast(I32), 0)
         nc.vector.memset(out_t[:], 0.0)
 
-        def load_scales(s0, s1):
-            for r in range(4):
+        def load_scales(s0, s1, rows=range(4)):
+            for r in rows:
                 nc.sync.dma_start(out=ws_t[r:P:32, s0 // N : s1 // N, :].bitcast(I32), in_=ws_rows[r:16:4, s0 // N : s1 // N])
 
         def load_weights(s0, s1):
@@ -75,7 +76,8 @@ def tile_moe_two_lin_gelu_kernel(tc, xT, w_words, w_scales, b, gate, offs, dst, 
             nc.sync.dma_start(out=raw[t][:], in_=x_rows[:, t, :])
             if t == 0:
                 nc.sync.dma_start(offs_t[:], offs)
-                load_scales(0, G)
+                load_scales(0, G, range(EARLY_ROWS))
+        load_scales(0, G, range(EARLY_ROWS, 4))
         load_weights(0, G)
         nc.sync.dma_start(bias[0], b[:, :EG])
         load_gate(0, G)

@@ -78,15 +78,16 @@ def tile_moe_two_lin_gelu_kernel(tc, xT, w_words, w_scales, b, gate, offs, dst, 
                 nc.sync.dma_start(offs_t[:], offs)
                 load_scales(0, G, range(EARLY_ROWS))
         load_scales(0, G, range(EARLY_ROWS, 4))
-        load_weights(0, G)
+        load_weights(0, G // 2)
+        load_weights(G // 2, G)
         nc.sync.dma_start(bias[0], b[:, :EG])
         load_gate(0, G)
         nc.sync.dma_start(dst_t[:], dst)
         load_scales(G, SLOTS)
         nc.sync.dma_start(bias[1], b[:, EG : 2 * EG])
-        for s0, s1 in ((G, 2 * G), (2 * G, SLOTS)):
-            load_weights(s0, s1)
-            load_gate(s0, s1)
+        load_weights(G, SLOTS)
+        load_gate(G, 2 * G)
+        load_gate(2 * G, SLOTS)
         nc.sync.dma_start(b_t[:], b[:, 2 * EG :])
 
         words = grouped[:].rearrange("p (n t) -> p n t", t=4)

import concourse.mybir as mybir

T, E, SLOTS, N = 4096, 16, 2048, 128
FLOPS = 2 * SLOTS * 512 * N

F32 = mybir.dt.float32
BF16 = mybir.dt.bfloat16
I32 = mybir.dt.int32
U32 = mybir.dt.uint32
U16 = mybir.dt.uint16
U8 = mybir.dt.uint8
FP8X4 = mybir.dt.float8_e4m3fn_x4
FP4X4 = mybir.dt.float4_e2m1fn_x4

P = 128
G = 512
EG = G // N
GROUPS = SLOTS // G

DIRECT = 1280
EARLY_ROWS = 2
SCALAR_FIRST = 64
SCALAR_SECOND = 96


def tile_moe_two_lin_gelu_kernel(tc, xT, w_words, w_scales, b, gate, offs, dst, out):
    nc = tc.nc
    gelu = mybir.ActivationFunctionType.Gelu_apprx_tanh
    copy = mybir.ActivationFunctionType.Copy
    mult = mybir.AluOpType.mult

    with tc.tile_pool(name="keep", bufs=1) as keep, tc.psum_pool(name="psum", bufs=1) as psum:
        offs_t = keep.tile([P, SLOTS // 16], U16, name="offs_t")
        dst_t = keep.tile([P, SLOTS // 16], U16, name="dst_t")
        raw = [keep.tile([P, T], F32, name=f"raw{t}") for t in range(4)]
        grouped = keep.tile([P, 4 * SLOTS], BF16, name="grouped", align_bytes=64)
        early = keep.tile([P, 2 * (SLOTS - DIRECT)], BF16, name="early")
        late = [keep.tile([P, 2 * G], BF16, name=f"late{g}") for g in range(GROUPS)]
        codes = keep.tile([P, SLOTS], U32, name="codes", align_bytes=64)
        scales = keep.tile([P, SLOTS], U8, name="scales", align_bytes=64)
        w_t = keep.tile([P, E, 2 * N], U8, name="w_t", align_bytes=64)
        ws_t = keep.tile([P, E, N], U8, name="ws_t", align_bytes=64)
        b_t = keep.tile([P, E - 2 * EG], F32, name="b_t")
        gate_t = keep.tile([P, SLOTS], F32, name="gate_t")
        y = keep.tile([P, SLOTS], F32, name="y")
        out_t = keep.tile([P, T], F32, name="out_t")
        warm = keep.tile([P, 1], F32, name="warm")
        first = [psum.tile([P, N], F32, name=f"first{e}") for e in range(EG)]
        later = [psum.tile([P, G], F32, name=f"later{g}") for g in range(3)]
        acc = [tile[:] for tile in first] + [tile[:, i * N : (i + 1) * N] for tile in later for i in range(EG)]

        x_rows = xT.rearrange("(p t) w -> p t w", t=4)
        ws_rows = w_scales.bitcast(I32).rearrange("e a q n -> (a q) e n")
        w_rows = w_words.bitcast(I32).rearrange("e a p n -> p (e a) n")

        middle = 3 * G // 4
        bias = [late[g + 2][:].bitcast(F32)[:, middle - EG // 2 : middle + EG // 2] for g in range(2)]
        bias = bias + [b_t[:, :EG], b_t[:, EG:]]

        nc.vector.memset(warm[:], 0.0)
        nc.scalar.activation(out=warm[:], in_=warm[:], func=gelu)
        nc.vector.memset(ws_t[:].rearrange("p e n -> p (e n)").bitcast(I32), 0)
        nc.vector.memset(out_t[:], 0.0)

        def load_scales(s0, s1, rows=range(4)):
            for r in rows:
                nc.sync.dma_start(out=ws_t[r:P:32, s0 // N : s1 // N, :].bitcast(I32), in_=ws_rows[r:16:4, s0 // N : s1 // N])

        def load_weights(s0, s1):
            nc.sync.dma_start(out=w_t[:, s0 // N : s1 // N, :].bitcast(I32), in_=w_rows[:, s0 // N : s1 // N, :])

        def load_gate(s0, s1):
            nc.sync.dma_start(out=gate_t[:, s0:s1], in_=gate[:, s0:s1])

        for t in range(4):
            nc.sync.dma_start(out=raw[t][:], in_=x_rows[:, t, :])
            if t == 0:
                nc.sync.dma_start(offs_t[:], offs)
                load_scales(0, G, range(EARLY_ROWS))
        load_scales(0, G, range(EARLY_ROWS, 4))
        load_weights(0, G // 2)
        load_weights(G // 2, G)
        nc.sync.dma_start(bias[0], b[:, :EG])
        load_gate(0, G)
        nc.sync.dma_start(dst_t[:], dst)
        load_scales(G, SLOTS)
        nc.sync.dma_start(bias[1], b[:, EG : 2 * EG])
        load_weights(G, SLOTS)
        load_gate(G, 2 * G)
        load_gate(2 * G, SLOTS)
        nc.sync.dma_start(b_t[:], b[:, 2 * EG :])

        words = grouped[:].rearrange("p (n t) -> p n t", t=4)

        def listed(t, s0, s1):
            return raw[t][:].indirect(offs_t[:, s0 // 16 : s1 // 16])

        def late_plane(t, s0, s1):
            c0 = (t - 2) * G + s0 % G
            return late[s0 // G][:, c0 : c0 + s1 - s0]

        def gather_vector(t, s0, s1):
            nc.vector.tensor_copy(late_plane(t, s0, s1), listed(t, s0, s1))

        def gather_scalar(t, s0, s1):
            nc.scalar.activation(late_plane(t, s0, s1), listed(t, s0, s1), copy)

        def place(move, s0, s1):
            pairs = late[s0 // G][:, : 2 * G].rearrange("p (u n) -> p n u", u=2)
            move(out=words[:, s0:s1, 2:4], in_=pairs[:, s0 % G : s0 % G + s1 - s0, :])

        def quantize_and_multiply(s0, s1):
            nc.vector.quantize_mx(out=codes[:, s0:s1].bitcast(FP8X4), scales=scales[:, s0:s1], in_=grouped[:, 4 * s0 : 4 * s1])
            for e in range(s0 // N, s1 // N):
                nc.tensor.matmul_mx(
                    out=acc[e],
                    lhsT=w_t[:, e, :].bitcast(FP4X4),
                    lhsT_scale=ws_t[:, e, :],
                    rhs=codes[:, e * N : (e + 1) * N].bitcast(FP8X4),
                    rhs_scale=scales[:, e * N : (e + 1) * N],
                    start=True,
                    stop=True,
                )

        def activate(g):
            for i in range(EG):
                e = g * EG + i
                nc.scalar.activation(out=y[:, e * N : (e + 1) * N], in_=acc[e], func=gelu, bias=bias[g][:, i : i + 1])

        def scatter(g):
            s0, s1 = g * G, (g + 1) * G
            nc.vector.tensor_tensor(out_t[:].indirect(dst_t[:, s0 // 16 : s1 // 16]), y[:, s0:s1], gate_t[:, s0:s1], mult)

        rest = SLOTS - DIRECT
        for t in range(2):
            nc.vector.tensor_copy(words[:, :DIRECT, t], listed(t, 0, DIRECT))
            nc.scalar.activation(early[:, t * rest : (t + 1) * rest], listed(t, DIRECT, SLOTS), copy)
        nc.scalar.copy(out=words[:, DIRECT:, 0:2], in_=early[:].rearrange("p (u n) -> p n u", u=2))
        for g in range(2):
            gather_vector(2, g * G, (g + 1) * G)
            gather_scalar(2, (g + 2) * G, (g + 3) * G)

        gather_vector(3, 0, N)
        gather_vector(3, N, 2 * N)
        gather_scalar(3, 2 * N, G)
        gather_scalar(3, G, G + G // 2)
        place(nc.scalar.copy, G - SCALAR_FIRST, G)
        gather_scalar(3, 2 * G - 2 * N, 2 * G - N)
        gather_scalar(3, 2 * G - N, 2 * G)
        place(nc.scalar.copy, G, G + SCALAR_SECOND)
        place(nc.vector.tensor_copy, 0, N)
        place(nc.vector.tensor_copy, N, 2 * N)
        place(nc.vector.tensor_copy, 2 * N, G - SCALAR_FIRST)
        for e in range(EG):
            quantize_and_multiply(e * N, (e + 1) * N)
        place(nc.vector.tensor_copy, G + SCALAR_SECOND, G + G // 2)
        place(nc.vector.tensor_copy, 2 * G - 2 * N, 2 * G - N)
        place(nc.vector.tensor_copy, 2 * G - N, 2 * G)
        quantize_and_multiply(G, G + G // 2)
        quantize_and_multiply(G + G // 2, 2 * G)
        activate(0)

        for g in range(GROUPS):
            halves = range((g + 2) * G, min(g + 3, GROUPS) * G, G // 2)
            for s0 in halves:
                gather_scalar(3, s0, s0 + G // 2)
            for s0 in halves:
                place(nc.scalar.copy, s0, s0 + G // 2)
            if g + 1 < GROUPS:
                activate(g + 1)
            scatter(g)
            for s0 in halves:
                quantize_and_multiply(s0, s0 + G // 2)
        nc.sync.dma_start(out, out_t[:])
